import numpy as np, ml_dtypes
CORES = [48,51,52,55]
N = 4
BF = ml_dtypes.bfloat16
M, Q, CAP, V = 4096, 384, 160, 16
R = 2 ** 20; H = R - 2 ** 13
def shave(lo, hi, u, k):
    return [lo[i] + int((hi[i] - lo[i]) * k * u[3 + i]) for i in range(3)] + [hi[i] - int((hi[i] - lo[i]) * k * u[6 + i]) for i in range(3)]
def scene(rng, h, deep, uneven):
    U = rng.random((M, 12)).tolist(); u = U[0]; side = [int(h * (1 + 0.5 * u[i])) for i in range(3)]
    lo = [int(u[3 + i] * (2 * h - side[i])) - h for i in range(3)]; hi = [lo[i] + side[i] for i in range(3)]
    box = [lo + hi] * M; skip = [M] * M; todo = [(1, M, lo, hi, M, V - 1)]
    while todo:
        a, b, lo, hi, out, v = todo.pop(); u = U[a]; s = b - a
        if s <= 4 or (s <= v and (deep or u[0] < 0.3)):
            for n in range(a, b):
                w = U[n]; box[n] = shave(lo, hi, w, 0.25)
                k = n + 1 if deep or w[2] < 0.5 else n + 1 + int(w[11] * (b - n)); skip[n] = k if k < b else out
            if out > b:
                i = int(u[1] * 3); box[b - 1][3 + i] = box[b - 1][i] - 1
            continue
        c = 5 * 2 ** (v - 5) - 1; x = max(2, s - 1 - c); z = min(s - 3, c)
        m = a + 1 + (V - 2 if deep and a == 1 else x + int(u[9] * (z - x + 1)))
        i = int(u[1] * 3); cut = lo[i] + int((hi[i] - lo[i]) * (0.25 + 0.5 * u[10]))
        l2 = lo[:]; l2[i] = min(cut + 1, hi[i]); h2 = hi[:]; h2[i] = cut
        yes, no = ((lo, h2), (l2, hi)) if u[2] < 0.5 else ((l2, hi), (lo, h2))
        box[a] = shave(yes[0], yes[1], u, 0.125); skip[a] = m
        todo += [(a + 1, m) + yes + (out, v - 1), (m, b) + no + (out, v - 1)]
    w = 2 ** rng.integers(0, 17, M) if uneven else rng.integers(1, 2 ** 16 + 1, M)
    return np.concatenate([np.array(box, np.int64).T, np.array([skip], np.int64), (w * (2 * rng.integers(0, 2, M) - 1))[None]])
def scenes(rng, h, deep=False, uneven=False):
    t = np.zeros((N, 8, 16, M), np.int64)
    for r in range(N):
        for g in range(8):
            t[r, g, :8] = scene(rng, int(h[g]), deep, uneven)
    return t
def points(rng, h):
    h = np.asarray(h, np.int64).reshape(1, 8, 1, 1); return rng.integers(-h, h + 1, (N, 8, 3, Q))
def inbox(t, p):
    return ((t[:, :3, :1] <= p) & (p <= t[:, 3:6, :1])).all(-2)
def far(rng, n):
    return rng.integers(R - 2 ** 12, R + 1, (3, n))
def made(rng, t, p, s=0):
    for r in range(N):
        for q in [(r + s + i) % N for i in range(N)]:
            if q == r: continue
            k = inbox(t[q], p[r])
            for g in range(8):
                i = rng.permutation(np.flatnonzero(k[g]))[CAP:]
                if len(i): p[r, g][:, i] = far(rng, len(i))
    return {"nodes": t.reshape(N, 128, M).astype(np.int32), "pts": p.reshape(N, 24, Q).astype(np.int32)}
def setup_inputs(rng):
    return made(rng, scenes(rng, [H] * 8), points(rng, [H] * 8))
def setup_inputs_faces(rng):
    t = scenes(rng, [H] * 8); p = np.zeros((N, 8, 3, Q), np.int64)
    for g in range(8):
        q = rng.integers(0, N, (N, 1, Q)); n = rng.integers(0, M, (N, 1, Q)) * (rng.random((N, 1, Q)) > 0.25)
        p[:, g] = t[q, g, np.arange(3)[:, None] + 3 * rng.integers(0, 2, (N, 3, Q)), n] + rng.integers(-1, 2, (N, 3, Q))
    return made(rng, t, p)
def setup_inputs_full(rng):
    t = scenes(rng, [H] * 8); p = points(rng, [H] * 8); s = int(rng.integers(1, N))
    for r in range(N):
        b = t[(r + s) % N, :, :6, :1]; p[r] = b[:, :3] + np.floor(rng.random((8, 3, Q)) * (b[:, 3:] - b[:, :3] + 1)).astype(np.int64)
    return made(rng, t, p, s)
def setup_inputs_few(rng):
    t = scenes(rng, [H] * 8); p = points(rng, [H] * 8); o = rng.permutation(N); b, c = o[:2]; e = o[2:]; t[e, :, 3, 0] = t[e, :, 0, 0] - 1
    w = t[c, :, :6, :1]; p[c] = w[:, :3] + np.floor(rng.random((8, 3, Q)) * (w[:, 3:] - w[:, :3] + 1)).astype(np.int64)
    for g in range(8):
        p[b, g] = far(rng, Q); v = t[b, g, :3, 0] + np.floor(rng.random(3) * (t[b, g, 3:6, 0] - t[b, g, :3, 0] + 1)).astype(np.int64)
        p[b, g, :, :4] = v[:, None]; p[b, g, :, Q - 4:] = v[:, None]
    return made(rng, t, p)
def setup_inputs_deep(rng):
    return made(rng, scenes(rng, [H] * 8, deep=True), points(rng, [H] * 8))
def setup_inputs_spread(rng):
    h = 2 ** rng.integers(5, 20, 8); p = points(rng, h)
    return made(rng, scenes(rng, h, uneven=True), p >> (rng.integers(0, 6, (N, 8, 1, Q)) * (rng.random((N, 8, 1, Q)) < 0.25)))
def walk(t, p):
    nd = t.transpose(0, 2, 1); x = p.transpose(0, 1, 3, 2); c = np.zeros((N, 8, Q), np.int64); s = np.zeros_like(c); v = np.zeros_like(c)
    while (c < M).any():
        live = c < M; b = nd[np.arange(8)[:, None], np.minimum(c, M - 1)]
        hit = live & (b[..., :3] <= x).all(-1) & (x <= b[..., 3:6]).all(-1)
        s += hit * b[..., 7]; v += live; c = np.where(live, np.where(hit, c + 1, b[..., 6]), c)
    return s, v
def check_inputs(d):
    t = d["nodes"].astype(np.int64).reshape(N, 8, 16, M); p = d["pts"].astype(np.int64).reshape(N, 8, 3, Q); k = t[:, :, 6]; bad = []
    if (k <= np.arange(M)).any() or (k > M).any() or (k[:, :, 0] != M).any(): return ["skips"]
    if np.abs(t[:, :, :6]).max() > R or np.abs(p).max() > R: bad.append("coordinates")
    if np.abs(t[:, :, 7]).max() > 2 ** 16: bad.append("weights")
    if t[:, :, 8:].any(): bad.append("rows of zeros")
    n = np.stack([np.sum(inbox(t[q], p), axis=-1) for q in range(N)])
    n[np.arange(N), np.arange(N)] = 0
    if n.max() > CAP: bad.append("points in another rank's first box")
    if max(walk(t[q], p)[1].max() for q in range(N)) > V: bad.append("visits")
    return bad
def reference(nodes, pts):
    t = nodes.astype(np.int64).reshape(N, 8, 16, M); p = pts.astype(np.int64).reshape(N, 8, 3, Q); y = np.zeros((N, 8, Q), np.int64)
    for q in range(N):
        y += walk(t[q], p)[0]
    return {"y": y.astype(np.float32)}

@@ -1,0 +1,348 @@
+from concourse.bass import DstId, RemoteDMATransfer
+from concourse.mybir import dt, AluOpType, AxisListType, ActivationFunctionType
+
+OP = AluOpType
+FN = ActivationFunctionType
+NB = 3
+NL = 512
+STEPS = 16
+M = 4096
+WIN = 4104
+WIN2 = 4112
+WC = 4
+BIG = 262144.0
+
+SCRATCH = {
+    "W": ("sbuf", [128, WIN], "int32"),
+    "W2": ("sbuf", [128, WIN2], "bfloat16"),
+    "Z": ("sbuf", [128, 512], "bfloat16"),
+    "X": ("sbuf", [128, 96], "int32"),
+    "X2": ("sbuf", [128, 512], "int32"),
+    "HI": ("sbuf", [128, 512], "bfloat16"),
+    "LO": ("sbuf", [128, 512], "bfloat16"),
+    "NHI": ("sbuf", [128, 512], "int32"),
+    "NHB": ("sbuf", [128, 512], "bfloat16"),
+    "NLB": ("sbuf", [128, 512], "bfloat16"),
+    "PR": ("sbuf", [128, 4 * 384], "int32"),
+    "CI": ("sbuf", [128, 128], "int32"),
+    "CJ": ("sbuf", [128, 128], "int32"),
+    "CG": ("sbuf", [128, 32], "int32"),
+    "CH": ("sbuf", [128, 32], "int32"),
+    "KI": ("sbuf", [128, 16], "int32"),
+    "KF": ("sbuf", [128, 64], "float32"),
+    "ID": ("sbuf", [128, 128], "bfloat16"),
+    "NID": ("sbuf", [128, 128], "bfloat16"),
+    "IDF": ("sbuf", [128, 128], "float32"),
+    "MASK": ("sbuf", [128, 128], "float32"),
+    "E1": ("sbuf", [128, 32], "float32"),
+    "E2": ("sbuf", [128, 32], "float32"),
+    "E3": ("sbuf", [128, 32], "float32"),
+    "SEL": ("sbuf", [128, 32], "float16"),
+    "RA": ("sbuf", [128, 96], "bfloat16"),
+    "RB": ("sbuf", [128, 64], "bfloat16"),
+    "OUT": ("sbuf", [128, 96], "float32"),
+    "TMP": ("sbuf", [128, 96], "float32"),
+    "SUM": ("sbuf", [128, 24], "float32"),
+    "YS": ("sbuf", [128, 128], "float32"),
+    "AC0": ("psum", [128, 512], "float32"),
+    "AC1": ("psum", [128, 512], "float32"),
+}
+for _b in range(NB):
+    SCRATCH["P%d" % _b] = ("sbuf", [128, NL], "int32")
+    SCRATCH["C%d" % _b] = ("sbuf", [128, NL], "bfloat16")
+    SCRATCH["G%d" % _b] = ("sbuf", [128, NL], "bfloat16")
+    SCRATCH["CU%d" % _b] = ("sbuf", [128, 32], "uint16")
+    SCRATCH["AM%d" % _b] = ("sbuf", [128, 128], "float16")
+    SCRATCH["IN%d" % _b] = ("sbuf", [128, 128], "float16")
+    SCRATCH["HW%d" % _b] = ("sbuf", [128, 128], "bfloat16")
+    SCRATCH["BK%d" % _b] = ("psum", [128, 512], "float32")
+    SCRATCH["CP%d" % _b] = ("psum", [128, 512], "float32")
+for _r in range(4):
+    SCRATCH["D%d" % _r] = ("dram", [128, 96], "int32")
+    SCRATCH["L%d" % _r] = ("sbuf", [128, 96], "float32")
+
+SEMAPHORES = ["xld", "x2ld", "wld", "fill", "fz", "f2", "fp", "v", "iot", "w2ld", "own", "psent", "rsent",
+              "lo", "oa", "fin", "fq", "yd", "hl", "go"]
+SEMAPHORES += ["fw%d" % c for c in range(WC)]
+for _b in range(NB):
+    SEMAPHORES += ["%s%d" % (n, _b) for n in ("cu", "cc", "gg", "mm", "mk", "mn", "ee", "hw", "ac")]
+for _r in range(4):
+    SEMAPHORES += ["pa%d" % _r, "pl%d" % _r, "ra%d" % _r]
+
+
+def rank_program(g, core, T, topo):
+    rank = T.rank_of(core)
+    if rank is None:
+        return
+    sem = T.sem
+    V, S, PE, Y = g.vector, g.scalar, g.tensor, g.sync
+    n_ranks = len(T.cores)
+    peers = [(rank + s) % n_ranks for s in range(1, n_ranks)]
+    dst_cores = [T.cores[r] for r in peers]
+    eng = topo.engines(core, dst_cores[0])[::2]
+    emask = sum(1 << e for e in eng)
+    ne = len(eng)
+    ids = []
+    for c in dst_cores:
+        rid, pid, _se = topo.addr(c)
+        ids.append(DstId(rid=rid, pnc=pid))
+
+    for a in range(4):
+        Y.dma_start(T.X[32 * a:32 * a + 32, :], T.pts[a % 3::3, :]).then_inc(sem.xld, 16)
+    Y.dma_start(T.X2[0:64, :], T.nodes[6::16, :]).then_inc(sem.x2ld, 16)
+    Y.dma_start(T.X2[64:128, :], T.nodes[7::16, :]).then_inc(sem.x2ld, 16)
+    Y.wait_ge(sem.fill, 1)
+    for a in range(6):
+        Y.dma_start(T.PR[a::16, 0:384], T.pts[a % 3::3, :]).then_inc(sem.own, 16)
+    w = M // WC
+    Y.wait_ge(sem.go, 1)
+    for c in range(WC):
+        Y.wait_ge(sem["fw%d" % c], 1)
+        for a in range(6):
+            Y.dma_start(T.W[a::16, w * c:w * c + w], T.nodes[a::16, w * c:w * c + w]).then_inc(sem.wld, 16)
+
+    g.iota(T.KI[:, 0:1], [[1, 1]], 0, 1).then_inc(sem.iot, 1)
+    g.iota(T.CI[:, :], [[1, 128]], 0, 0).then_inc(sem.iot, 1)
+    g.iota(T.PR[:, 0:768], [[0, 192], [1, 4]], 0, 0).then_inc(sem.fill, 1)
+    g.wait_ge(sem.xld, 64)
+    g.remote_dma_fused([RemoteDMATransfer(dst_ids=ids, dma_engine_mask=emask, remote_sem=sem["pa%d" % rank],
+                                          src=T.X[:, :], dsts=[T["D%d" % rank][:, :] for _ in ids])],
+                       local_sem=sem.psent)
+    g.sem_inc(sem.go, 1)
+    g.iota(T.PR[:, 768:1536], [[0, 192], [1, 4]], 0, 0).then_inc(sem.fp, 1)
+    g.iota(T.NHI[0:64, :], [[1, 16], [0, 32]], 0, 16).then_inc(sem.iot, 1)
+    g.iota(T.NLB[0:64, :], [[0, 16], [1, 32]], 1, 0, allow_small_or_imprecise_dtypes=True).then_inc(sem.iot, 1)
+
+    S.wait_ge(sem.fz, 1)
+    for c in range(8):
+        S.activation(T.W2[:, c * 512:c * 512 + 512], T.Z[:, :], FN.Copy).then_inc(sem.f2, 1)
+
+    nv = [0]
+
+    def v(ins):
+        nv[0] += 1
+        ins.then_inc(sem.v, 1)
+
+    def vsync():
+        V.wait_ge(sem.v, nv[0])
+
+    KF = T.KF
+
+    def col(j):
+        return KF[:, j:j + 1]
+
+    v(V.memset(T.Z[:, :], 0.0))
+    v(V.memset(KF[:, :], 0.0))
+    V.wait_ge(sem.iot, 2)
+    v(V.tensor_scalar(T.KI[:, 1:2], T.KI[:, 0:1], 15, None, OP.bitwise_and))
+    v(V.tensor_scalar(T.KI[:, 2:3], T.KI[:, 0:1], 4, None, OP.arith_shift_right))
+    v(V.tensor_scalar(T.KI[:, 3:4], T.KI[:, 0:1], 3, None, OP.bitwise_and))
+    v(V.tensor_scalar(T.KI[:, 4:5], T.KI[:, 0:1], 2, None, OP.arith_shift_right))
+    v(V.tensor_scalar(T.KI[:, 5:6], T.KI[:, 0:1], 3, None, OP.arith_shift_right))
+    vsync()
+    v(V.tensor_copy(KF[:, 0:6], T.KI[:, 0:6]))
+    vsync()
+    p_, r_, g_, i_, k_ = [col(j) for j in range(5)]
+    v(V.tensor_scalar(col(14), r_, 14.0, None, OP.is_equal))
+    vsync()
+    V.tensor_scalar(T.Z[:, :], T.Z[:, :], col(14), None, OP.add).then_inc(sem.fz, 1)
+    for c in range(WC):
+        V.memset(T.W[:, w * c:w * c + w], 0).then_inc(sem["fw%d" % c], 1)
+    v(V.memset(T.W2[:, M:WIN2], 1.0))
+    v(V.memset(T.W[:, M:WIN], 0))
+    for b in range(NB):
+        V.memset(T["CU%d" % b][:, :], 0).then_inc(sem["cu%d" % b], 1)
+
+    V.wait_ge(sem.x2ld, 32)
+    v(V.tensor_copy(T.HI[:, :], T.X2[:, :]))
+    vsync()
+    v(V.tensor_tensor(T.LO[:, :], T.X2[:, :], T.HI[:, :], OP.subtract))
+    hilo = nv[0]
+    v(V.tensor_scalar(col(6), col(5), 128.0, None, OP.mult))
+    V.wait_ge(sem.iot, 4)
+    vsync()
+    v(V.tensor_scalar(T.NHB[0:64, :], T.NHI[0:64, :], KF[0:64, 6:7], None, OP.subtract))
+    nhb = nv[0]
+
+    v(V.tensor_scalar(T.CJ[:, :], T.CI[:, :], 2, 3, OP.arith_shift_right, OP.bitwise_and))
+    v(V.tensor_scalar(T.CG[:, :], T.CI[:, 0:32], 2, None, OP.arith_shift_right))
+    v(V.tensor_scalar(T.CH[:, :], T.CI[:, 0:32], 7, None, OP.bitwise_and))
+    v(V.tensor_scalar(col(7), r_, 3.0, 2.0, OP.is_lt, OP.mult))
+    v(V.tensor_scalar(col(8), r_, 6.0, None, OP.is_lt))
+    v(V.tensor_scalar(col(25), r_, 6.0, 3.0, OP.is_equal, OP.mult))
+    for base, terms in ((16, [(6, 1.0), (8, 1.0), (14, -2048.0), (12, 4096.0), (13, -2.0)]),
+                        (30, [(10, 32.0), (11, 1.0), (12, 8192.0)]),
+                        (34, [(6, -7.0), (7, 9.0), (9, -1.0), (10, -2.0), (11, -7.0)])):
+        for n, (row, c) in enumerate(terms):
+            v(V.tensor_scalar(col(base + n), r_, float(row), c, OP.is_equal, OP.mult))
+    v(V.tensor_scalar(col(39), r_, 3.0, -1.0, OP.is_ge, OP.mult))
+    v(V.tensor_scalar(col(22), r_, 7.0, None, OP.is_equal))
+    v(V.tensor_scalar(col(23), r_, 9.0, None, OP.is_equal))
+    v(V.tensor_scalar(col(24), r_, 12.0, None, OP.is_equal))
+    v(V.tensor_scalar(col(40), r_, 8.0, None, OP.subtract))
+    v(V.tensor_scalar(col(41), r_, 7.0, None, OP.subtract))
+    vsync()
+    v(V.tensor_reduce(col(15), KF[:, 34:40], AxisListType.X, OP.add))
+    v(V.tensor_tensor(col(9), col(7), col(8), OP.subtract))
+    v(V.tensor_reduce(col(10), KF[:, 16:21], AxisListType.X, OP.add))
+    v(V.tensor_reduce(col(21), KF[:, 30:33], AxisListType.X, OP.add))
+    v(V.tensor_tensor(col(11), col(22), col(24), OP.subtract))
+    v(V.tensor_tensor(col(12), col(23), col(24), OP.subtract))
+    v(V.tensor_scalar(T.E1[:, :], T.CJ[:, 0:128:4], col(40), None, OP.is_equal))
+    v(V.tensor_scalar(T.E2[:, :], T.CJ[:, 0:128:4], col(41), None, OP.is_equal))
+    vsync()
+    v(V.tensor_tensor(col(13), col(9), col(25), OP.add))
+    v(V.tensor_scalar(col(26), col(11), -1.0, None, OP.mult))
+    v(V.tensor_scalar(col(27), col(12), -1.0, None, OP.mult))
+    v(V.tensor_tensor(T.E3[:, :], T.E2[:, :], T.E1[:, :], OP.subtract))
+    v(V.tensor_scalar(T.MASK[:, :], T.CJ[:, :], i_, None, OP.is_equal))
+    v(V.tensor_scalar(T.ID[:, :], T.CI[:, :], p_, None, OP.is_equal))
+    v(V.tensor_scalar(T.NID[:, :], T.CI[:, :], p_, -1.0, OP.is_equal, OP.mult))
+    v(V.tensor_scalar(T.SEL[:, :], T.CI[:, 0:32], k_, None, OP.is_equal))
+    v(V.tensor_scalar(T.RA[:, 0:32], T.CG[:, :], g_, col(10), OP.is_equal, OP.mult))
+    v(V.tensor_scalar(T.RA[:, 64:96], T.CG[:, :], g_, col(21), OP.is_equal, OP.mult))
+    vsync()
+    v(V.tensor_scalar(col(28), col(13), 8192.0, None, OP.mult))
+    v(V.tensor_scalar(col(29), col(13), -BIG, None, OP.mult))
+    v(V.tensor_scalar(T.E1[:, :], T.CG[:, :], g_, 2048.0, OP.is_equal, OP.mult))
+    for n, c in enumerate((11, 12, 26, 27)):
+        v(V.tensor_scalar(T.RA[:, 32 + 8 * n:40 + 8 * n], T.CI[:, 0:8], g_, col(c), OP.is_equal, OP.mult))
+    vsync()
+    v(V.tensor_scalar(T.E2[:, :], T.CG[:, :], g_, col(28), OP.is_equal, OP.mult))
+    v(V.tensor_tensor(T.E1[:, :], T.E1[:, :], T.E3[:, :], OP.mult))
+    v(V.tensor_scalar(T.RB[:, 0:32], T.CH[:, :], g_, col(29), OP.is_equal, OP.mult))
+    vsync()
+    v(V.tensor_tensor(T.RB[:, 32:64], T.E1[:, :], T.E2[:, :], OP.add))
+    statics = nv[0]
+
+    S.wait_ge(sem.f2, 8)
+    S.wait_ge(sem.v, hilo)
+    S.dma_start(T.W2[6::16, 0:M], T.HI[0:64, :]).then_inc(sem.w2ld, 16)
+    S.dma_start(T.W2[7::16, 0:M], T.HI[64:128, :]).then_inc(sem.w2ld, 16)
+    S.dma_start(T.W2[8::16, 0:M], T.LO[0:64, :]).then_inc(sem.w2ld, 16)
+    S.dma_start(T.W2[9::16, 0:M], T.LO[64:128, :]).then_inc(sem.w2ld, 16)
+    S.wait_ge(sem.iot, 4)
+    S.dma_start(T.W2[11::16, 0:M], T.NLB[0:64, :]).then_inc(sem.w2ld, 16)
+    S.wait_ge(sem.v, nhb)
+    S.dma_start(T.W2[10::16, 0:M], T.NHB[0:64, :]).then_inc(sem.w2ld, 16)
+
+    Y.wait_ge(sem.fp, 1)
+    for s, r in enumerate(peers):
+        Y.wait_ge(sem["pa%d" % r], ne)
+        for a in range(6):
+            Y.dma_start(T.PR[a::16, 384 * (s + 1):384 * (s + 2)],
+                        T["D%d" % r][32 * (a % 3):32 * (a % 3) + 32, :]).then_inc(sem["pl%d" % r], 16)
+
+    for s in range(n_ranks):
+        if s == 0:
+            V.wait_ge(sem.own, 96)
+        else:
+            V.wait_ge(sem["pl%d" % peers[s - 1]], 96)
+        for b in range(NB):
+            v(V.tensor_scalar(T["P%d" % b][:, s::4], T.PR[:, 384 * s + 128 * b:384 * s + 128 * b + 128],
+                              col(15), None, OP.add))
+    vsync()
+
+    V.wait_ge(sem.wld, 16 * 6 * WC)
+    S.wait_ge(sem.w2ld, 96)
+    PE.wait_ge(sem.v, statics)
+
+    def gather(x):
+        t, b = divmod(x, NB)
+        B = str(b)
+        V.wait_ge(sem["cu" + B], t + 1)
+        V.tensor_tensor(T["C" + B][:, :], T.W[:, 0:WIN].indirect(T["CU" + B][:, :]), T["P" + B][:, :], OP.is_gt
+                        ).then_inc(sem["cc" + B], 1)
+        S.wait_ge(sem["cu" + B], t + 1)
+        S.activation(T["G" + B][:, :], T.W2[:, 0:WIN2].indirect(T["CU" + B][:, :]), FN.Copy).then_inc(sem["gg" + B], 1)
+        bank = T["BK" + B]
+        PE.wait_ge(sem["gg" + B], t + 1)
+        for i in range(4):
+            PE.matmul(bank[:, i:384:4], T["G" + B][:, i::4], T.RA[:, :], i == 0, False).then_inc(sem["mm" + B], 1)
+        PE.wait_ge(sem["cc" + B], t + 1)
+        for i in range(4):
+            PE.matmul(bank[:, 128 + i:384:4], T["C" + B][:, i::4], T.RB[:, :], False, i == 3).then_inc(sem["mm" + B], 1)
+
+    def move(x):
+        t, b = divmod(x, NB)
+        B = str(b)
+        bank = T["BK" + B]
+        if t == STEPS - 1:
+            return
+        V.wait_ge(sem["mm" + B], 8 * (t + 1))
+        V.tensor_tensor(T["AM" + B][:, :], bank[:, 0:128], T.MASK[:, :], OP.mult).then_inc(sem["mk" + B], 1)
+        V.wait_ge(sem["mk" + B], t + 1)
+        V.tensor_tensor(T["IN" + B][:, :], bank[:, 256:384], T["AM" + B][:, :], OP.min).then_inc(sem["mn" + B], 1)
+        PE.wait_ge(sem["mn" + B], t + 1)
+        PE.matmul(T["CP" + B][:, 0:32], T["IN" + B][:, :], T.SEL[:, :], True, True).then_inc(sem["ee" + B], 1)
+
+    def cast(x):
+        t, b = divmod(x, NB)
+        B = str(b)
+        if t == STEPS - 1:
+            return
+        V.wait_ge(sem["ee" + B], t + 1)
+        V.tensor_scalar(T["CU" + B][:, :], T["CP" + B][:, 0:32], 2048.0, None, OP.add).then_inc(sem["cu" + B], 1)
+
+    def acc(b):
+        return T.AC1[:, 0:64] if b == NB - 1 else T.AC0[:, 64 * b:64 * b + 64]
+
+    def weigh(x):
+        t, b = divmod(x, NB)
+        B = str(b)
+        if t == STEPS - 1:
+            S.wait_ge(sem["mm" + B], 8 * (t + 1))
+        else:
+            S.wait_ge(sem["mn" + B], t + 1)
+        if t:
+            S.wait_ge(sem["ac" + B], 2 * t)
+        S.activation(T["HW" + B][:, :], T["BK" + B][:, 128:256], FN.Relu).then_inc(sem["hw" + B], 1)
+        PE.wait_ge(sem["hw" + B], t + 1)
+        PE.matmul(acc(b), T.ID[:, :], T["HW" + B][:, 0:64], t == 0 and b != 1, False).then_inc(sem["ac" + B], 1)
+        PE.matmul(acc(b), T.NID[:, :], T["HW" + B][:, 64:128], False, t == STEPS - 1 and b != 0
+                  ).then_inc(sem["ac" + B], 1)
+
+    total = NB * STEPS
+    for x in range(total + 2):
+        if x < total:
+            gather(x)
+        if 0 <= x - 2 < total:
+            cast(x - 2)
+        if 0 <= x - 1 < total:
+            move(x - 1)
+        if 0 <= x - 2 < total:
+            weigh(x - 2)
+
+    v(V.tensor_scalar(T.IDF[:, :], T.CI[:, :], p_, None, OP.is_equal))
+    idf = nv[0]
+    for b in range(NB):
+        for bb in ([0, 1] if b < NB - 1 else [2]):
+            S.wait_ge(sem["ac%d" % bb], 2 * STEPS)
+            V.wait_ge(sem["ac%d" % bb], 2 * STEPS)
+        S.activation(T.TMP[:, 32 * b:32 * b + 32], acc(b)[:, 32:64], FN.Copy).then_inc(sem.lo, 1)
+        V.wait_ge(sem.lo, max(b + 1, 2))
+        V.tensor_tensor(T.OUT[:, 32 * b:32 * b + 32], acc(b)[:, 0:32], T.TMP[:, 32 * b:32 * b + 32], OP.add
+                        ).then_inc(sem.oa, 1)
+    g.wait_ge(sem.oa, NB)
+    g.remote_dma_fused([RemoteDMATransfer(dst_ids=ids, dma_engine_mask=emask, remote_sem=sem["ra%d" % rank],
+                                          src=T.OUT[:, :], dsts=[T["L%d" % rank][:, :] for _ in ids])],
+                       local_sem=sem.rsent)
+    V.wait_ge(sem.oa, NB)
+    prev = T.OUT[:, 0::4]
+    for s, r in enumerate(peers):
+        V.wait_ge(sem["ra%d" % r], ne)
+        if s:
+            V.wait_ge(sem.fin, s)
+        V.tensor_tensor(T.SUM[:, :], prev, T["L%d" % r][:, (rank - r) % n_ranks::4], OP.add).then_inc(sem.fin, 1)
+        prev = T.SUM[:, :]
+    PE.wait_ge(sem.v, idf)
+    PE.wait_ge(sem.fin, 3)
+    PE.matmul(T.BK0[0:24, 0:128], T.SUM[:, :], T.IDF[:, :], True, True).then_inc(sem.fq, 1)
+    V.wait_ge(sem.fq, 1)
+    V.tensor_copy(T.YS[0:24, :], T.BK0[0:24, 0:128]).then_inc(sem.hl, 1)
+    for b, q in enumerate((Y, S, Y)):
+        q.wait_ge(sem.hl, 1)
+        q.dma_start(T.y[:, 128 * b:128 * b + 128], T.YS[8 * b:8 * b + 8, :]).then_inc(sem.yd, 16)
+    Y.wait_ge(sem.yd, 48)
+    g.wait_ge(sem.psent, ne)
+    g.wait_ge(sem.rsent, ne)

@@ -10,17 +10,21 @@ M = 4096
 WIN = 4104
 WIN2 = 4112
 WC = 4
+EPD = 4
 BIG = 262144.0
 
 SCRATCH = {
     "W": ("sbuf", [128, WIN], "int32"),
     "W2": ("sbuf", [128, WIN2], "bfloat16"),
     "Z": ("sbuf", [128, 512], "bfloat16"),
-    "X": ("sbuf", [128, 96], "int32"),
+    "X": ("dram", [128, 96], "int32"),
+    "N0": ("sbuf", [128, 2], "int32"),
+    "P": ("sbuf", [128, NB * NL], "int32"),
+    "CM": ("sbuf", [128, 128], "float32"),
+    "CQ": ("sbuf", [128, 128], "float32"),
     "X2": ("sbuf", [128, 512], "int32"),
     "HI": ("sbuf", [128, 512], "bfloat16"),
     "LO": ("sbuf", [128, 512], "bfloat16"),
-    "NHI": ("sbuf", [128, 512], "int32"),
     "NHB": ("sbuf", [128, 512], "bfloat16"),
     "NLB": ("sbuf", [128, 512], "bfloat16"),
     "PR": ("sbuf", [128, 4 * 384], "int32"),
@@ -29,6 +33,7 @@ SCRATCH = {
     "CG": ("sbuf", [128, 32], "int32"),
     "CH": ("sbuf", [128, 32], "int32"),
     "KI": ("sbuf", [128, 16], "int32"),
+    "KB": ("sbuf", [128, 8], "float32"),
     "KF": ("sbuf", [128, 64], "float32"),
     "ID": ("sbuf", [128, 128], "bfloat16"),
     "NID": ("sbuf", [128, 128], "bfloat16"),
@@ -48,7 +53,6 @@ SCRATCH = {
     "AC1": ("psum", [128, 512], "float32"),
 }
 for _b in range(NB):
-    SCRATCH["P%d" % _b] = ("sbuf", [128, NL], "int32")
     SCRATCH["C%d" % _b] = ("sbuf", [128, NL], "bfloat16")
     SCRATCH["G%d" % _b] = ("sbuf", [128, NL], "bfloat16")
     SCRATCH["CU%d" % _b] = ("sbuf", [128, 32], "uint16")
@@ -59,11 +63,11 @@ for _b in range(NB):
     SCRATCH["CP%d" % _b] = ("psum", [128, 512], "float32")
 for _r in range(4):
     SCRATCH["D%d" % _r] = ("dram", [128, 96], "int32")
-    SCRATCH["L%d" % _r] = ("sbuf", [128, 96], "float32")
+    SCRATCH["L%d" % _r] = ("sbuf", [128, 24], "float32")
 
-SEMAPHORES = ["xld", "x2ld", "wld", "fill", "fz", "f2", "fp", "v", "iot", "w2ld", "own", "psent", "rsent",
-              "lo", "oa", "fin", "fq", "yd", "hl", "go"]
-SEMAPHORES += ["fw%d" % c for c in range(WC)]
+SEMAPHORES = ["xld", "x2ld", "fill", "fz", "f2", "fp", "v", "iot", "w2ld", "own", "psent", "rsent",
+              "lo", "oa", "fin", "fq", "yd", "hl", "n0", "nb"]
+SEMAPHORES += ["fw%d" % c for c in range(WC)] + ["wl%d" % c for c in range(WC)]
 for _b in range(NB):
     SEMAPHORES += ["%s%d" % (n, _b) for n in ("cu", "cc", "gg", "mm", "mk", "mn", "ee", "hw", "ac")]
 for _r in range(4):
@@ -78,40 +82,48 @@ def rank_program(g, core, T, topo):
     V, S, PE, Y = g.vector, g.scalar, g.tensor, g.sync
     n_ranks = len(T.cores)
     peers = [(rank + s) % n_ranks for s in range(1, n_ranks)]
-    dst_cores = [T.cores[r] for r in peers]
-    eng = topo.engines(core, dst_cores[0])[::2]
-    emask = sum(1 << e for e in eng)
-    ne = len(eng)
-    ids = []
-    for c in dst_cores:
+
+    order = sorted(range(1, n_ranks), key=lambda s: topo.die(T.cores[(rank + s) % n_ranks]) == topo.die(core))
+    dests = []
+    for n, s in enumerate(order):
+        c = T.cores[(rank + s) % n_ranks]
+        e = topo.engines(core, c)
+        e = (e[0::2] + e[1::2])[EPD * n:EPD * n + EPD]
         rid, pid, _se = topo.addr(c)
-        ids.append(DstId(rid=rid, pnc=pid))
+        dests.append((s, DstId(rid=rid, pnc=pid), sum(1 << x for x in e)))
 
     for a in range(4):
         Y.dma_start(T.X[32 * a:32 * a + 32, :], T.pts[a % 3::3, :]).then_inc(sem.xld, 16)
     Y.dma_start(T.X2[0:64, :], T.nodes[6::16, :]).then_inc(sem.x2ld, 16)
     Y.dma_start(T.X2[64:128, :], T.nodes[7::16, :]).then_inc(sem.x2ld, 16)
+    Y.dma_start(T.N0[:, :], T.nodes[:, 0:2]).then_inc(sem.n0, 16)
     Y.wait_ge(sem.fill, 1)
     for a in range(6):
         Y.dma_start(T.PR[a::16, 0:384], T.pts[a % 3::3, :]).then_inc(sem.own, 16)
+    Y.wait_ge(sem.fp, 1)
+    for s, r in enumerate(peers):
+        Y.wait_ge(sem["pa%d" % r], EPD)
+        for a in range(6):
+            Y.dma_start(T.PR[a::16, 384 * (s + 1):384 * (s + 2)],
+                        T["D%d" % r][32 * (a % 3):32 * (a % 3) + 32, :]).then_inc(sem["pl%d" % r], 16)
     w = M // WC
-    Y.wait_ge(sem.go, 1)
     for c in range(WC):
         Y.wait_ge(sem["fw%d" % c], 1)
         for a in range(6):
-            Y.dma_start(T.W[a::16, w * c:w * c + w], T.nodes[a::16, w * c:w * c + w]).then_inc(sem.wld, 16)
+            Y.dma_start(T.W[a::16, w * c:w * c + w], T.nodes[a::16, w * c:w * c + w]).then_inc(sem["wl%d" % c], 16)
 
     g.iota(T.KI[:, 0:1], [[1, 1]], 0, 1).then_inc(sem.iot, 1)
     g.iota(T.CI[:, :], [[1, 128]], 0, 0).then_inc(sem.iot, 1)
-    g.iota(T.PR[:, 0:768], [[0, 192], [1, 4]], 0, 0).then_inc(sem.fill, 1)
+    g.iota(T.PR[:, 0:384], [[0, 96], [1, 4]], 0, 0).then_inc(sem.fill, 1)
     g.wait_ge(sem.xld, 64)
-    g.remote_dma_fused([RemoteDMATransfer(dst_ids=ids, dma_engine_mask=emask, remote_sem=sem["pa%d" % rank],
-                                          src=T.X[:, :], dsts=[T["D%d" % rank][:, :] for _ in ids])],
+    g.remote_dma_fused([RemoteDMATransfer(dst_ids=[d], dma_engine_mask=m, remote_sem=sem["pa%d" % rank],
+                                          src=T.X[:, :], dst=T["D%d" % rank][:, :]) for s, d, m in dests],
                        local_sem=sem.psent)
-    g.sem_inc(sem.go, 1)
-    g.iota(T.PR[:, 768:1536], [[0, 192], [1, 4]], 0, 0).then_inc(sem.fp, 1)
-    g.iota(T.NHI[0:64, :], [[1, 16], [0, 32]], 0, 16).then_inc(sem.iot, 1)
-    g.iota(T.NLB[0:64, :], [[0, 16], [1, 32]], 1, 0, allow_small_or_imprecise_dtypes=True).then_inc(sem.iot, 1)
+    g.iota(T.CM[:, :], [[0, 4], [1, 32]], 1, 0, allow_small_or_imprecise_dtypes=True).then_inc(sem.iot, 1)
+    g.iota(T.CQ[:, :], [[1, 4], [0, 32]], 0, 0, allow_small_or_imprecise_dtypes=True).then_inc(sem.iot, 1)
+    g.iota(T.PR[:, 384:1536], [[0, 288], [1, 4]], 0, 0).then_inc(sem.fp, 1)
+    for c in range(2, WC):
+        g.iota(T.W[:, w * c:w * c + w], [[0, w]], 0, 0).then_inc(sem["fw%d" % c], 1)
 
     S.wait_ge(sem.fz, 1)
     for c in range(8):
@@ -138,15 +150,16 @@ def rank_program(g, core, T, topo):
     v(V.tensor_scalar(T.KI[:, 2:3], T.KI[:, 0:1], 4, None, OP.arith_shift_right))
     v(V.tensor_scalar(T.KI[:, 3:4], T.KI[:, 0:1], 3, None, OP.bitwise_and))
     v(V.tensor_scalar(T.KI[:, 4:5], T.KI[:, 0:1], 2, None, OP.arith_shift_right))
-    v(V.tensor_scalar(T.KI[:, 5:6], T.KI[:, 0:1], 3, None, OP.arith_shift_right))
+    v(V.tensor_scalar(T.KI[:, 5:6], T.KI[:, 0:1], 7, None, OP.bitwise_and))
     vsync()
     v(V.tensor_copy(KF[:, 0:6], T.KI[:, 0:6]))
     vsync()
+    base = nv[0]
     p_, r_, g_, i_, k_ = [col(j) for j in range(5)]
     v(V.tensor_scalar(col(14), r_, 14.0, None, OP.is_equal))
     vsync()
     V.tensor_scalar(T.Z[:, :], T.Z[:, :], col(14), None, OP.add).then_inc(sem.fz, 1)
-    for c in range(WC):
+    for c in range(2):
         V.memset(T.W[:, w * c:w * c + w], 0).then_inc(sem["fw%d" % c], 1)
     v(V.memset(T.W2[:, M:WIN2], 1.0))
     v(V.memset(T.W[:, M:WIN], 0))
@@ -158,11 +171,6 @@ def rank_program(g, core, T, topo):
     vsync()
     v(V.tensor_tensor(T.LO[:, :], T.X2[:, :], T.HI[:, :], OP.subtract))
     hilo = nv[0]
-    v(V.tensor_scalar(col(6), col(5), 128.0, None, OP.mult))
-    V.wait_ge(sem.iot, 4)
-    vsync()
-    v(V.tensor_scalar(T.NHB[0:64, :], T.NHI[0:64, :], KF[0:64, 6:7], None, OP.subtract))
-    nhb = nv[0]
 
     v(V.tensor_scalar(T.CJ[:, :], T.CI[:, :], 2, 3, OP.arith_shift_right, OP.bitwise_and))
     v(V.tensor_scalar(T.CG[:, :], T.CI[:, 0:32], 2, None, OP.arith_shift_right))
@@ -170,11 +178,11 @@ def rank_program(g, core, T, topo):
     v(V.tensor_scalar(col(7), r_, 3.0, 2.0, OP.is_lt, OP.mult))
     v(V.tensor_scalar(col(8), r_, 6.0, None, OP.is_lt))
     v(V.tensor_scalar(col(25), r_, 6.0, 3.0, OP.is_equal, OP.mult))
-    for base, terms in ((16, [(6, 1.0), (8, 1.0), (14, -2048.0), (12, 4096.0), (13, -2.0)]),
-                        (30, [(10, 32.0), (11, 1.0), (12, 8192.0)]),
-                        (34, [(6, -7.0), (7, 9.0), (9, -1.0), (10, -2.0), (11, -7.0)])):
+    for at, terms in ((16, [(6, 1.0), (8, 1.0), (14, -2048.0), (12, 4096.0), (13, -2.0)]),
+                      (30, [(10, 32.0), (11, 1.0), (12, 8192.0)]),
+                      (34, [(6, -7.0), (7, 9.0), (9, -1.0), (10, -2.0), (11, -7.0)])):
         for n, (row, c) in enumerate(terms):
-            v(V.tensor_scalar(col(base + n), r_, float(row), c, OP.is_equal, OP.mult))
+            v(V.tensor_scalar(col(at + n), r_, float(row), c, OP.is_equal, OP.mult))
     v(V.tensor_scalar(col(39), r_, 3.0, -1.0, OP.is_ge, OP.mult))
     v(V.tensor_scalar(col(22), r_, 7.0, None, OP.is_equal))
     v(V.tensor_scalar(col(23), r_, 9.0, None, OP.is_equal))
@@ -213,6 +221,9 @@ def rank_program(g, core, T, topo):
     v(V.tensor_scalar(T.RB[:, 0:32], T.CH[:, :], g_, col(29), OP.is_equal, OP.mult))
     vsync()
     v(V.tensor_tensor(T.RB[:, 32:64], T.E1[:, :], T.E2[:, :], OP.add))
+    V.wait_ge(sem.n0, 16)
+    for n in range(2):
+        v(V.tensor_tensor(col(42 + n), T.N0[:, n:n + 1], col(8), OP.mult))
     statics = nv[0]
 
     S.wait_ge(sem.f2, 8)
@@ -221,38 +232,43 @@ def rank_program(g, core, T, topo):
     S.dma_start(T.W2[7::16, 0:M], T.HI[64:128, :]).then_inc(sem.w2ld, 16)
     S.dma_start(T.W2[8::16, 0:M], T.LO[0:64, :]).then_inc(sem.w2ld, 16)
     S.dma_start(T.W2[9::16, 0:M], T.LO[64:128, :]).then_inc(sem.w2ld, 16)
+    S.wait_ge(sem.v, base)
     S.wait_ge(sem.iot, 4)
+    for u in range(4):
+        S.activation(T.KB[0:64, u:u + 1], KF[0:64, 5:6], FN.Copy, bias=4.0 * u, scale=16.0).then_inc(sem.nb, 1)
+        S.activation(T.NLB[0:64, 128 * u:128 * u + 128], T.CM[0:64, :], FN.Copy).then_inc(sem.nb, 1)
+    S.wait_ge(sem.nb, 8)
     S.dma_start(T.W2[11::16, 0:M], T.NLB[0:64, :]).then_inc(sem.w2ld, 16)
-    S.wait_ge(sem.v, nhb)
+    for u in range(4):
+        S.activation(T.NHB[0:64, 128 * u:128 * u + 128], T.CQ[0:64, :], FN.Identity, bias=T.KB[0:64, u:u + 1]
+                     ).then_inc(sem.nb, 1)
+    S.wait_ge(sem.nb, 12)
     S.dma_start(T.W2[10::16, 0:M], T.NHB[0:64, :]).then_inc(sem.w2ld, 16)
-
-    Y.wait_ge(sem.fp, 1)
-    for s, r in enumerate(peers):
-        Y.wait_ge(sem["pa%d" % r], ne)
-        for a in range(6):
-            Y.dma_start(T.PR[a::16, 384 * (s + 1):384 * (s + 2)],
-                        T["D%d" % r][32 * (a % 3):32 * (a % 3) + 32, :]).then_inc(sem["pl%d" % r], 16)
 
     for s in range(n_ranks):
         if s == 0:
             V.wait_ge(sem.own, 96)
         else:
             V.wait_ge(sem["pl%d" % peers[s - 1]], 96)
-        for b in range(NB):
-            v(V.tensor_scalar(T["P%d" % b][:, s::4], T.PR[:, 384 * s + 128 * b:384 * s + 128 * b + 128],
-                              col(15), None, OP.add))
+        v(V.tensor_scalar(T.P[:, s::4], T.PR[:, 384 * s:384 * s + 384], col(15), None, OP.add))
     vsync()
 
-    V.wait_ge(sem.wld, 16 * 6 * WC)
     S.wait_ge(sem.w2ld, 96)
     PE.wait_ge(sem.v, statics)
 
     def gather(x):
         t, b = divmod(x, NB)
         B = str(b)
+        points = T.P[:, NL * b:NL * b + NL]
+        if x == 2 * NB:
+            for c in range(WC):
+                V.wait_ge(sem["wl%d" % c], 96)
         V.wait_ge(sem["cu" + B], t + 1)
-        V.tensor_tensor(T["C" + B][:, :], T.W[:, 0:WIN].indirect(T["CU" + B][:, :]), T["P" + B][:, :], OP.is_gt
-                        ).then_inc(sem["cc" + B], 1)
+        if t < 2:
+            V.tensor_scalar(T["C" + B][:, :], points, col(42 + t), None, OP.is_lt).then_inc(sem["cc" + B], 1)
+        else:
+            V.tensor_tensor(T["C" + B][:, :], T.W[:, 0:WIN].indirect(T["CU" + B][:, :]), points, OP.is_gt
+                            ).then_inc(sem["cc" + B], 1)
         S.wait_ge(sem["cu" + B], t + 1)
         S.activation(T["G" + B][:, :], T.W2[:, 0:WIN2].indirect(T["CU" + B][:, :]), FN.Copy).then_inc(sem["gg" + B], 1)
         bank = T["BK" + B]
@@ -321,19 +337,20 @@ def rank_program(g, core, T, topo):
             V.wait_ge(sem["ac%d" % bb], 2 * STEPS)
         S.activation(T.TMP[:, 32 * b:32 * b + 32], acc(b)[:, 32:64], FN.Copy).then_inc(sem.lo, 1)
         V.wait_ge(sem.lo, max(b + 1, 2))
-        V.tensor_tensor(T.OUT[:, 32 * b:32 * b + 32], acc(b)[:, 0:32], T.TMP[:, 32 * b:32 * b + 32], OP.add
-                        ).then_inc(sem.oa, 1)
-    g.wait_ge(sem.oa, NB)
-    g.remote_dma_fused([RemoteDMATransfer(dst_ids=ids, dma_engine_mask=emask, remote_sem=sem["ra%d" % rank],
-                                          src=T.OUT[:, :], dsts=[T["L%d" % rank][:, :] for _ in ids])],
-                       local_sem=sem.rsent)
-    V.wait_ge(sem.oa, NB)
-    prev = T.OUT[:, 0::4]
-    for s, r in enumerate(peers):
-        V.wait_ge(sem["ra%d" % r], ne)
-        if s:
-            V.wait_ge(sem.fin, s)
-        V.tensor_tensor(T.SUM[:, :], prev, T["L%d" % r][:, (rank - r) % n_ranks::4], OP.add).then_inc(sem.fin, 1)
+        for s in range(n_ranks):
+            V.tensor_tensor(T.OUT[:, 24 * s + 8 * b:24 * s + 8 * b + 8], acc(b)[:, s:32:4],
+                            T.TMP[:, 32 * b + s:32 * b + 32:4], OP.add).then_inc(sem.oa, 1)
+    g.wait_ge(sem.oa, NB * n_ranks)
+    g.remote_dma_fused([RemoteDMATransfer(dst_ids=[d], dma_engine_mask=m, remote_sem=sem["ra%d" % rank],
+                                          src=T.OUT[:, 24 * s:24 * s + 24], dst=T["L%d" % rank][:, :])
+                        for s, d, m in dests], local_sem=sem.rsent)
+    V.wait_ge(sem.oa, NB * n_ranks)
+    prev = T.OUT[:, 0:24]
+    for n, r in enumerate(peers):
+        V.wait_ge(sem["ra%d" % r], EPD)
+        if n:
+            V.wait_ge(sem.fin, n)
+        V.tensor_tensor(T.SUM[:, :], prev, T["L%d" % r][:, :], OP.add).then_inc(sem.fin, 1)
         prev = T.SUM[:, :]
     PE.wait_ge(sem.v, idf)
     PE.wait_ge(sem.fin, 3)
@@ -344,5 +361,5 @@ def rank_program(g, core, T, topo):
         q.wait_ge(sem.hl, 1)
         q.dma_start(T.y[:, 128 * b:128 * b + 128], T.YS[8 * b:8 * b + 8, :]).then_inc(sem.yd, 16)
     Y.wait_ge(sem.yd, 48)
-    g.wait_ge(sem.psent, ne)
-    g.wait_ge(sem.rsent, ne)
+    g.wait_ge(sem.psent, 3 * EPD)
+    g.wait_ge(sem.rsent, 3 * EPD)

@@ -5,7 +5,7 @@ OP = AluOpType
 FN = ActivationFunctionType
 NB = 3
 NL = 512
-STEPS = 16
+STEPS = 15
 M = 4096
 WIN = 4104
 WIN2 = 4112
@@ -19,6 +19,7 @@ SCRATCH = {
     "Z": ("sbuf", [128, 512], "bfloat16"),
     "X": ("dram", [128, 96], "int32"),
     "N0": ("sbuf", [128, 2], "int32"),
+    "KV": ("sbuf", [128, 4], "bfloat16"),
     "P": ("sbuf", [128, NB * NL], "int32"),
     "CM": ("sbuf", [128, 128], "float32"),
     "CQ": ("sbuf", [128, 128], "float32"),
@@ -39,12 +40,17 @@ SCRATCH = {
     "NID": ("sbuf", [128, 128], "bfloat16"),
     "IDF": ("sbuf", [128, 128], "float32"),
     "MASK": ("sbuf", [128, 128], "float32"),
+    "B32": ("sbuf", [128, 32], "float32"),
+    "B8": ("sbuf", [128, 32], "float32"),
     "E1": ("sbuf", [128, 32], "float32"),
     "E2": ("sbuf", [128, 32], "float32"),
     "E3": ("sbuf", [128, 32], "float32"),
+    "E5": ("sbuf", [128, 32], "float32"),
     "SEL": ("sbuf", [128, 32], "float16"),
     "RA": ("sbuf", [128, 96], "bfloat16"),
     "RB": ("sbuf", [128, 64], "bfloat16"),
+    "R0": ("sbuf", [128, 128], "bfloat16"),
+    "R1": ("sbuf", [128, 96], "bfloat16"),
     "OUT": ("sbuf", [128, 96], "float32"),
     "TMP": ("sbuf", [128, 96], "float32"),
     "SUM": ("sbuf", [128, 24], "float32"),
@@ -59,6 +65,7 @@ for _b in range(NB):
     SCRATCH["AM%d" % _b] = ("sbuf", [128, 128], "float16")
     SCRATCH["IN%d" % _b] = ("sbuf", [128, 128], "float16")
     SCRATCH["HW%d" % _b] = ("sbuf", [128, 128], "bfloat16")
+    SCRATCH["HX%d" % _b] = ("sbuf", [128, 128], "bfloat16")
     SCRATCH["BK%d" % _b] = ("psum", [128, 512], "float32")
     SCRATCH["CP%d" % _b] = ("psum", [128, 512], "float32")
 for _r in range(4):
@@ -66,7 +73,7 @@ for _r in range(4):
     SCRATCH["L%d" % _r] = ("sbuf", [128, 24], "float32")
 
 SEMAPHORES = ["xld", "x2ld", "fill", "fz", "f2", "fp", "v", "iot", "w2ld", "own", "psent", "rsent",
-              "lo", "oa", "fin", "fq", "yd", "hl", "n0", "nb"]
+              "lo", "oa", "fin", "fq", "yd", "hl", "n0", "nb", "go", "kv", "rr", "rs"]
 SEMAPHORES += ["fw%d" % c for c in range(WC)] + ["wl%d" % c for c in range(WC)]
 for _b in range(NB):
     SEMAPHORES += ["%s%d" % (n, _b) for n in ("cu", "cc", "gg", "mm", "mk", "mn", "ee", "hw", "ac")]
@@ -100,17 +107,23 @@ def rank_program(g, core, T, topo):
     Y.wait_ge(sem.fill, 1)
     for a in range(6):
         Y.dma_start(T.PR[a::16, 0:384], T.pts[a % 3::3, :]).then_inc(sem.own, 16)
+    w = M // WC
+
+    def load(c):
+        Y.wait_ge(sem["fw%d" % c], 1)
+        for a in range(6):
+            Y.dma_start(T.W[a::16, w * c:w * c + w], T.nodes[a::16, w * c:w * c + w]).then_inc(sem["wl%d" % c], 16)
+
+    Y.wait_ge(sem.go, 1)
+    load(0)
     Y.wait_ge(sem.fp, 1)
     for s, r in enumerate(peers):
         Y.wait_ge(sem["pa%d" % r], EPD)
         for a in range(6):
             Y.dma_start(T.PR[a::16, 384 * (s + 1):384 * (s + 2)],
                         T["D%d" % r][32 * (a % 3):32 * (a % 3) + 32, :]).then_inc(sem["pl%d" % r], 16)
-    w = M // WC
-    for c in range(WC):
-        Y.wait_ge(sem["fw%d" % c], 1)
-        for a in range(6):
-            Y.dma_start(T.W[a::16, w * c:w * c + w], T.nodes[a::16, w * c:w * c + w]).then_inc(sem["wl%d" % c], 16)
+    load(1)
+    load(2)
 
     g.iota(T.KI[:, 0:1], [[1, 1]], 0, 1).then_inc(sem.iot, 1)
     g.iota(T.CI[:, :], [[1, 128]], 0, 0).then_inc(sem.iot, 1)
@@ -119,15 +132,12 @@ def rank_program(g, core, T, topo):
     g.remote_dma_fused([RemoteDMATransfer(dst_ids=[d], dma_engine_mask=m, remote_sem=sem["pa%d" % rank],
                                           src=T.X[:, :], dst=T["D%d" % rank][:, :]) for s, d, m in dests],
                        local_sem=sem.psent)
-    g.iota(T.CM[:, :], [[0, 4], [1, 32]], 1, 0, allow_small_or_imprecise_dtypes=True).then_inc(sem.iot, 1)
+    g.sem_inc(sem.go, 1)
+    g.iota(T.CM[:, :], [[0, 4], [1, 32]], -1, 0, allow_small_or_imprecise_dtypes=True).then_inc(sem.iot, 1)
     g.iota(T.CQ[:, :], [[1, 4], [0, 32]], 0, 0, allow_small_or_imprecise_dtypes=True).then_inc(sem.iot, 1)
     g.iota(T.PR[:, 384:1536], [[0, 288], [1, 4]], 0, 0).then_inc(sem.fp, 1)
     for c in range(2, WC):
         g.iota(T.W[:, w * c:w * c + w], [[0, w]], 0, 0).then_inc(sem["fw%d" % c], 1)
-
-    S.wait_ge(sem.fz, 1)
-    for c in range(8):
-        S.activation(T.W2[:, c * 512:c * 512 + 512], T.Z[:, :], FN.Copy).then_inc(sem.f2, 1)
 
     nv = [0]
 
@@ -145,6 +155,7 @@ def rank_program(g, core, T, topo):
 
     v(V.memset(T.Z[:, :], 0.0))
     v(V.memset(KF[:, :], 0.0))
+    v(V.memset(T.KV[:, :], 0.0))
     V.wait_ge(sem.iot, 2)
     v(V.tensor_scalar(T.KI[:, 1:2], T.KI[:, 0:1], 15, None, OP.bitwise_and))
     v(V.tensor_scalar(T.KI[:, 2:3], T.KI[:, 0:1], 4, None, OP.arith_shift_right))
@@ -159,91 +170,129 @@ def rank_program(g, core, T, topo):
     v(V.tensor_scalar(col(14), r_, 14.0, None, OP.is_equal))
     vsync()
     V.tensor_scalar(T.Z[:, :], T.Z[:, :], col(14), None, OP.add).then_inc(sem.fz, 1)
-    for c in range(2):
-        V.memset(T.W[:, w * c:w * c + w], 0).then_inc(sem["fw%d" % c], 1)
-    v(V.memset(T.W2[:, M:WIN2], 1.0))
-    v(V.memset(T.W[:, M:WIN], 0))
-    for b in range(NB):
-        V.memset(T["CU%d" % b][:, :], 0).then_inc(sem["cu%d" % b], 1)
+    V.memset(T.W[:, 0:w], 0).then_inc(sem.fw0, 1)
 
     V.wait_ge(sem.x2ld, 32)
     v(V.tensor_copy(T.HI[:, :], T.X2[:, :]))
     vsync()
     v(V.tensor_tensor(T.LO[:, :], T.X2[:, :], T.HI[:, :], OP.subtract))
     hilo = nv[0]
+    V.memset(T.W[:, w:2 * w], 0).then_inc(sem.fw1, 1)
+    v(V.memset(T.W2[:, M:WIN2], 1.0))
+    v(V.memset(T.W[:, M:WIN], 0))
 
     v(V.tensor_scalar(T.CJ[:, :], T.CI[:, :], 2, 3, OP.arith_shift_right, OP.bitwise_and))
     v(V.tensor_scalar(T.CG[:, :], T.CI[:, 0:32], 2, None, OP.arith_shift_right))
     v(V.tensor_scalar(T.CH[:, :], T.CI[:, 0:32], 7, None, OP.bitwise_and))
     v(V.tensor_scalar(col(7), r_, 3.0, 2.0, OP.is_lt, OP.mult))
     v(V.tensor_scalar(col(8), r_, 6.0, None, OP.is_lt))
-    v(V.tensor_scalar(col(25), r_, 6.0, 3.0, OP.is_equal, OP.mult))
+    v(V.tensor_scalar(col(25), r_, 12.0, 3.0, OP.is_equal, OP.mult))
     for at, terms in ((16, [(6, 1.0), (8, 1.0), (14, -2048.0), (12, 4096.0), (13, -2.0)]),
                       (30, [(10, 32.0), (11, 1.0), (12, 8192.0)]),
-                      (34, [(6, -7.0), (7, 9.0), (9, -1.0), (10, -2.0), (11, -7.0)])):
+                      (37, [(14, -1.0), (15, 1.0)])):
         for n, (row, c) in enumerate(terms):
             v(V.tensor_scalar(col(at + n), r_, float(row), c, OP.is_equal, OP.mult))
+    v(V.tensor_scalar(col(34), r_, -1.0, 9.0, OP.mult, OP.add))
+    v(V.tensor_scalar(col(35), r_, 6.0, None, OP.is_ge))
     v(V.tensor_scalar(col(39), r_, 3.0, -1.0, OP.is_ge, OP.mult))
     v(V.tensor_scalar(col(22), r_, 7.0, None, OP.is_equal))
     v(V.tensor_scalar(col(23), r_, 9.0, None, OP.is_equal))
     v(V.tensor_scalar(col(24), r_, 12.0, None, OP.is_equal))
-    v(V.tensor_scalar(col(40), r_, 8.0, None, OP.subtract))
-    v(V.tensor_scalar(col(41), r_, 7.0, None, OP.subtract))
+    v(V.tensor_scalar(col(40), r_, 9.0, None, OP.subtract))
+    v(V.tensor_scalar(col(41), r_, 8.0, None, OP.subtract))
     vsync()
-    v(V.tensor_reduce(col(15), KF[:, 34:40], AxisListType.X, OP.add))
+    v(V.tensor_tensor(col(36), col(34), col(35), OP.mult))
     v(V.tensor_tensor(col(9), col(7), col(8), OP.subtract))
     v(V.tensor_reduce(col(10), KF[:, 16:21], AxisListType.X, OP.add))
     v(V.tensor_reduce(col(21), KF[:, 30:33], AxisListType.X, OP.add))
     v(V.tensor_tensor(col(11), col(22), col(24), OP.subtract))
     v(V.tensor_tensor(col(12), col(23), col(24), OP.subtract))
-    v(V.tensor_scalar(T.E1[:, :], T.CJ[:, 0:128:4], col(40), None, OP.is_equal))
-    v(V.tensor_scalar(T.E2[:, :], T.CJ[:, 0:128:4], col(41), None, OP.is_equal))
+    v(V.tensor_scalar(T.E1[:, :], T.CJ[:, 0:128:4], col(40), 2048.0, OP.is_equal, OP.mult))
+    v(V.tensor_scalar(T.E2[:, :], T.CJ[:, 0:128:4], col(41), 2048.0, OP.is_equal, OP.mult))
+    v(V.tensor_scalar(T.B32[:, :], T.CG[:, :], g_, None, OP.is_equal))
+    v(V.tensor_scalar(T.B8[:, :], T.CH[:, :], g_, None, OP.is_equal))
     vsync()
+    v(V.tensor_tensor(col(15), col(36), col(39), OP.add))
     v(V.tensor_tensor(col(13), col(9), col(25), OP.add))
     v(V.tensor_scalar(col(26), col(11), -1.0, None, OP.mult))
     v(V.tensor_scalar(col(27), col(12), -1.0, None, OP.mult))
+    v(V.tensor_scalar(col(54), col(38), -1.0, None, OP.mult))
     v(V.tensor_tensor(T.E3[:, :], T.E2[:, :], T.E1[:, :], OP.subtract))
-    v(V.tensor_scalar(T.MASK[:, :], T.CJ[:, :], i_, None, OP.is_equal))
-    v(V.tensor_scalar(T.ID[:, :], T.CI[:, :], p_, None, OP.is_equal))
-    v(V.tensor_scalar(T.NID[:, :], T.CI[:, :], p_, -1.0, OP.is_equal, OP.mult))
-    v(V.tensor_scalar(T.SEL[:, :], T.CI[:, 0:32], k_, None, OP.is_equal))
-    v(V.tensor_scalar(T.RA[:, 0:32], T.CG[:, :], g_, col(10), OP.is_equal, OP.mult))
-    v(V.tensor_scalar(T.RA[:, 64:96], T.CG[:, :], g_, col(21), OP.is_equal, OP.mult))
     vsync()
     v(V.tensor_scalar(col(28), col(13), 8192.0, None, OP.mult))
     v(V.tensor_scalar(col(29), col(13), -BIG, None, OP.mult))
-    v(V.tensor_scalar(T.E1[:, :], T.CG[:, :], g_, 2048.0, OP.is_equal, OP.mult))
-    for n, c in enumerate((11, 12, 26, 27)):
-        v(V.tensor_scalar(T.RA[:, 32 + 8 * n:40 + 8 * n], T.CI[:, 0:8], g_, col(c), OP.is_equal, OP.mult))
+    v(V.tensor_tensor(T.E5[:, :], T.E3[:, :], T.B32[:, :], OP.mult))
     vsync()
-    v(V.tensor_scalar(T.E2[:, :], T.CG[:, :], g_, col(28), OP.is_equal, OP.mult))
-    v(V.tensor_tensor(T.E1[:, :], T.E1[:, :], T.E3[:, :], OP.mult))
-    v(V.tensor_scalar(T.RB[:, 0:32], T.CH[:, :], g_, col(29), OP.is_equal, OP.mult))
-    vsync()
-    v(V.tensor_tensor(T.RB[:, 32:64], T.E1[:, :], T.E2[:, :], OP.add))
+    half = nv[0]
+    v(V.tensor_tensor(col(53), col(28), col(20), OP.subtract))
     V.wait_ge(sem.n0, 16)
     for n in range(2):
         v(V.tensor_tensor(col(42 + n), T.N0[:, n:n + 1], col(8), OP.mult))
+    V.wait_ge(sem.kv, 64)
+    v(V.tensor_tensor(col(52), T.KV[:, 1:2], col(18), OP.add))
+    for n, c in enumerate((14, 38, 37, 54)):
+        v(V.tensor_scalar(KF[:, 44 + 2 * n:46 + 2 * n], T.KV[:, 2:4], col(c), col(29), OP.mult, OP.add))
+    vsync()
+    v(V.tensor_scalar(T.E2[:, :], T.B32[:, :], col(53), None, OP.mult))
+    vsync()
+    v(V.tensor_tensor(T.RB[:, 32:64], T.E5[:, :], T.E2[:, :], OP.add))
+    cols = nv[0]
+    v(V.tensor_scalar(T.MASK[:, :], T.CJ[:, :], i_, None, OP.is_equal))
+    v(V.tensor_scalar(T.IDF[:, :], T.CI[:, :], p_, None, OP.is_equal))
+    v(V.tensor_scalar(T.SEL[:, :], T.CI[:, 0:32], k_, None, OP.is_equal))
     statics = nv[0]
 
-    S.wait_ge(sem.f2, 8)
+    S.wait_ge(sem.fz, 1)
+    for c in range(3):
+        S.activation(T.W2[:, c * 512:c * 512 + 512], T.Z[:, :], FN.Copy).then_inc(sem.f2, 1)
     S.wait_ge(sem.v, hilo)
-    S.dma_start(T.W2[6::16, 0:M], T.HI[0:64, :]).then_inc(sem.w2ld, 16)
-    S.dma_start(T.W2[7::16, 0:M], T.HI[64:128, :]).then_inc(sem.w2ld, 16)
-    S.dma_start(T.W2[8::16, 0:M], T.LO[0:64, :]).then_inc(sem.w2ld, 16)
-    S.dma_start(T.W2[9::16, 0:M], T.LO[64:128, :]).then_inc(sem.w2ld, 16)
+    for row, c, src in ((12, 0, T.HI[0:64:8, 0:2]), (13, 0, T.LO[0:64:8, 0:2]),
+                        (14, 2, T.HI[64:128:8, 0:2]), (15, 2, T.LO[64:128:8, 0:2])):
+        S.dma_start(T.KV[row::16, c:c + 2], src).then_inc(sem.kv, 16)
     S.wait_ge(sem.v, base)
     S.wait_ge(sem.iot, 4)
     for u in range(4):
         S.activation(T.KB[0:64, u:u + 1], KF[0:64, 5:6], FN.Copy, bias=4.0 * u, scale=16.0).then_inc(sem.nb, 1)
         S.activation(T.NLB[0:64, 128 * u:128 * u + 128], T.CM[0:64, :], FN.Copy).then_inc(sem.nb, 1)
     S.wait_ge(sem.nb, 8)
-    S.dma_start(T.W2[11::16, 0:M], T.NLB[0:64, :]).then_inc(sem.w2ld, 16)
     for u in range(4):
         S.activation(T.NHB[0:64, 128 * u:128 * u + 128], T.CQ[0:64, :], FN.Identity, bias=T.KB[0:64, u:u + 1]
                      ).then_inc(sem.nb, 1)
-    S.wait_ge(sem.nb, 12)
-    S.dma_start(T.W2[10::16, 0:M], T.NHB[0:64, :]).then_inc(sem.w2ld, 16)
+    for c in range(3, 8):
+        S.activation(T.W2[:, c * 512:c * 512 + 512], T.Z[:, :], FN.Copy).then_inc(sem.f2, 1)
+    nr = {"rr": 0, "rs": 0}
+
+    def scaled(name, out, mask, c):
+        nr[name] += 1
+        S.activation(out, mask, FN.Copy, scale=1.0 if c is None else col(c)).then_inc(sem[name], 1)
+
+    S.wait_ge(sem.v, half)
+    scaled("rr", T.R0[:, 0:32], T.B32[:, :], 28)
+    scaled("rr", T.R0[:, 32:64], T.B8[:, :], 29)
+    scaled("rr", T.R0[:, 64:96], T.B32[:, :], 28)
+    S.wait_ge(sem.v, cols)
+    for n in range(4):
+        scaled("rr", T.R0[:, 96 + 8 * n:104 + 8 * n], T.B8[:, 0:8], 44 + 2 * n)
+        scaled("rr", T.R1[:, 32 + 8 * n:40 + 8 * n], T.B8[:, 0:8], 45 + 2 * n)
+    scaled("rr", T.R1[:, 0:32], T.B32[:, :], 52)
+    scaled("rr", T.R1[:, 64:96], T.RB[:, 32:64], None)
+    S.wait_ge(sem.v, statics)
+    scaled("rs", T.ID[:, :], T.IDF[:, :], None)
+    nr["rs"] += 1
+    S.activation(T.NID[:, :], T.IDF[:, :], FN.Copy, scale=-1.0).then_inc(sem.rs, 1)
+    scaled("rs", T.RA[:, 0:32], T.B32[:, :], 10)
+    scaled("rs", T.RA[:, 64:96], T.B32[:, :], 21)
+    for n, c in enumerate((11, 12, 26, 27)):
+        scaled("rs", T.RA[:, 32 + 8 * n:40 + 8 * n], T.B8[:, 0:8], c)
+    scaled("rs", T.RB[:, 0:32], T.B8[:, :], 29)
+
+    Y.wait_ge(sem.nb, 12)
+    Y.wait_ge(sem.f2, 8)
+    Y.wait_ge(sem.v, hilo)
+    for row, src in ((6, T.HI[0:64, :]), (7, T.HI[64:128, :]), (8, T.LO[0:64, :]), (9, T.LO[64:128, :]),
+                     (11, T.NLB[0:64, :]), (10, T.NHB[0:64, :])):
+        Y.dma_start(T.W2[row::16, 0:M], src).then_inc(sem.w2ld, 16)
+    load(3)
 
     for s in range(n_ranks):
         if s == 0:
@@ -253,31 +302,39 @@ def rank_program(g, core, T, topo):
         v(V.tensor_scalar(T.P[:, s::4], T.PR[:, 384 * s:384 * s + 384], col(15), None, OP.add))
     vsync()
 
-    S.wait_ge(sem.w2ld, 96)
     PE.wait_ge(sem.v, statics)
+    PE.wait_ge(sem.rr, nr["rr"])
 
     def gather(x):
         t, b = divmod(x, NB)
         B = str(b)
         points = T.P[:, NL * b:NL * b + NL]
-        if x == 2 * NB:
+        bank = T["BK" + B]
+        C, G = T["C" + B], T["G" + B]
+        if t == 0:
+            V.tensor_scalar(G[:, :], points, col(42), None, OP.is_lt).then_inc(sem["cc" + B], 1)
+            V.tensor_scalar(C[:, :], points, col(43), None, OP.is_lt).then_inc(sem["cc" + B], 1)
+            PE.wait_ge(sem["cc" + B], 1)
+            for i in range(4):
+                PE.matmul(bank[:, i:512:4], G[:, i::4], T.R0[:, :], i == 0, False).then_inc(sem["mm" + B], 1)
+            PE.wait_ge(sem["cc" + B], 2)
+            for i in range(4):
+                PE.matmul(bank[:, i:384:4], C[:, i::4], T.R1[:, :], False, i == 3).then_inc(sem["mm" + B], 1)
+            return
+        if x == NB:
             for c in range(WC):
                 V.wait_ge(sem["wl%d" % c], 96)
-        V.wait_ge(sem["cu" + B], t + 1)
-        if t < 2:
-            V.tensor_scalar(T["C" + B][:, :], points, col(42 + t), None, OP.is_lt).then_inc(sem["cc" + B], 1)
-        else:
-            V.tensor_tensor(T["C" + B][:, :], T.W[:, 0:WIN].indirect(T["CU" + B][:, :]), points, OP.is_gt
-                            ).then_inc(sem["cc" + B], 1)
-        S.wait_ge(sem["cu" + B], t + 1)
-        S.activation(T["G" + B][:, :], T.W2[:, 0:WIN2].indirect(T["CU" + B][:, :]), FN.Copy).then_inc(sem["gg" + B], 1)
-        bank = T["BK" + B]
-        PE.wait_ge(sem["gg" + B], t + 1)
+            S.wait_ge(sem.w2ld, 96)
+        V.wait_ge(sem["cu" + B], t)
+        V.tensor_tensor(C[:, :], T.W[:, 0:WIN].indirect(T["CU" + B][:, :]), points, OP.is_gt).then_inc(sem["cc" + B], 1)
+        S.wait_ge(sem["cu" + B], t)
+        S.activation(G[:, :], T.W2[:, 0:WIN2].indirect(T["CU" + B][:, :]), FN.Copy).then_inc(sem["gg" + B], 1)
+        PE.wait_ge(sem["gg" + B], t)
         for i in range(4):
-            PE.matmul(bank[:, i:384:4], T["G" + B][:, i::4], T.RA[:, :], i == 0, False).then_inc(sem["mm" + B], 1)
-        PE.wait_ge(sem["cc" + B], t + 1)
+            PE.matmul(bank[:, i:384:4], G[:, i::4], T.RA[:, :], i == 0, False).then_inc(sem["mm" + B], 1)
+        PE.wait_ge(sem["cc" + B], t + 2)
         for i in range(4):
-            PE.matmul(bank[:, 128 + i:384:4], T["C" + B][:, i::4], T.RB[:, :], False, i == 3).then_inc(sem["mm" + B], 1)
+            PE.matmul(bank[:, 128 + i:384:4], C[:, i::4], T.RB[:, :], False, i == 3).then_inc(sem["mm" + B], 1)
 
     def move(x):
         t, b = divmod(x, NB)
@@ -298,7 +355,8 @@ def rank_program(g, core, T, topo):
         if t == STEPS - 1:
             return
         V.wait_ge(sem["ee" + B], t + 1)
-        V.tensor_scalar(T["CU" + B][:, :], T["CP" + B][:, 0:32], 2048.0, None, OP.add).then_inc(sem["cu" + B], 1)
+        V.tensor_scalar(T["CU" + B][:, :], T["CP" + B][:, 0:32], 2048.0, float(M), OP.add, OP.min
+                        ).then_inc(sem["cu" + B], 1)
 
     def acc(b):
         return T.AC1[:, 0:64] if b == NB - 1 else T.AC0[:, 64 * b:64 * b + 64]
@@ -311,12 +369,18 @@ def rank_program(g, core, T, topo):
         else:
             S.wait_ge(sem["mn" + B], t + 1)
         if t:
-            S.wait_ge(sem["ac" + B], 2 * t)
+            S.wait_ge(sem["ac" + B], 2 + 2 * t)
+        todo = [T["HW" + B]]
         S.activation(T["HW" + B][:, :], T["BK" + B][:, 128:256], FN.Relu).then_inc(sem["hw" + B], 1)
-        PE.wait_ge(sem["hw" + B], t + 1)
-        PE.matmul(acc(b), T.ID[:, :], T["HW" + B][:, 0:64], t == 0 and b != 1, False).then_inc(sem["ac" + B], 1)
-        PE.matmul(acc(b), T.NID[:, :], T["HW" + B][:, 64:128], False, t == STEPS - 1 and b != 0
-                  ).then_inc(sem["ac" + B], 1)
+        if t == 0:
+            todo.append(T["HX" + B])
+            S.activation(T["HX" + B][:, :], T["BK" + B][:, 384:512], FN.Relu).then_inc(sem["hw" + B], 1)
+        if x == 0:
+            PE.wait_ge(sem.rs, nr["rs"])
+        PE.wait_ge(sem["hw" + B], t + 2)
+        for n, h in enumerate(todo):
+            PE.matmul(acc(b), T.ID[:, :], h[:, 0:64], t == 0 and n == 0 and b != 1, False).then_inc(sem["ac" + B], 1)
+            PE.matmul(acc(b), T.NID[:, :], h[:, 64:128], False, t == STEPS - 1 and b != 0).then_inc(sem["ac" + B], 1)
 
     total = NB * STEPS
     for x in range(total + 2):
@@ -329,12 +393,10 @@ def rank_program(g, core, T, topo):
         if 0 <= x - 2 < total:
             weigh(x - 2)
 
-    v(V.tensor_scalar(T.IDF[:, :], T.CI[:, :], p_, None, OP.is_equal))
-    idf = nv[0]
     for b in range(NB):
         for bb in ([0, 1] if b < NB - 1 else [2]):
-            S.wait_ge(sem["ac%d" % bb], 2 * STEPS)
-            V.wait_ge(sem["ac%d" % bb], 2 * STEPS)
+            S.wait_ge(sem["ac%d" % bb], 2 + 2 * STEPS)
+            V.wait_ge(sem["ac%d" % bb], 2 + 2 * STEPS)
         S.activation(T.TMP[:, 32 * b:32 * b + 32], acc(b)[:, 32:64], FN.Copy).then_inc(sem.lo, 1)
         V.wait_ge(sem.lo, max(b + 1, 2))
         for s in range(n_ranks):
@@ -352,7 +414,6 @@ def rank_program(g, core, T, topo):
             V.wait_ge(sem.fin, n)
         V.tensor_tensor(T.SUM[:, :], prev, T["L%d" % r][:, :], OP.add).then_inc(sem.fin, 1)
         prev = T.SUM[:, :]
-    PE.wait_ge(sem.v, idf)
     PE.wait_ge(sem.fin, 3)
     PE.matmul(T.BK0[0:24, 0:128], T.SUM[:, :], T.IDF[:, :], True, True).then_inc(sem.fq, 1)
     V.wait_ge(sem.fq, 1)

@@ -12,6 +12,7 @@ WIN2 = 4112
 WC = 4
 EPD = 4
 BIG = 262144.0
+TOP = 57344.0
 
 SCRATCH = {
     "W": ("sbuf", [128, WIN], "int32"),
@@ -40,13 +41,11 @@ SCRATCH = {
     "NID": ("sbuf", [128, 128], "bfloat16"),
     "IDF": ("sbuf", [128, 128], "float32"),
     "MASK": ("sbuf", [128, 128], "float32"),
+    "FIT": ("sbuf", [128, 256], "float32"),
     "B32": ("sbuf", [128, 32], "float32"),
     "B8": ("sbuf", [128, 32], "float32"),
-    "E1": ("sbuf", [128, 32], "float32"),
-    "E2": ("sbuf", [128, 32], "float32"),
-    "E3": ("sbuf", [128, 32], "float32"),
-    "E5": ("sbuf", [128, 32], "float32"),
     "SEL": ("sbuf", [128, 32], "float16"),
+    "NSEL": ("sbuf", [128, 32], "float16"),
     "RA": ("sbuf", [128, 96], "bfloat16"),
     "RB": ("sbuf", [128, 64], "bfloat16"),
     "R0": ("sbuf", [128, 128], "bfloat16"),
@@ -62,8 +61,7 @@ for _b in range(NB):
     SCRATCH["C%d" % _b] = ("sbuf", [128, NL], "bfloat16")
     SCRATCH["G%d" % _b] = ("sbuf", [128, NL], "bfloat16")
     SCRATCH["CU%d" % _b] = ("sbuf", [128, 32], "uint16")
-    SCRATCH["AM%d" % _b] = ("sbuf", [128, 128], "float16")
-    SCRATCH["IN%d" % _b] = ("sbuf", [128, 128], "float16")
+    SCRATCH["IN%d" % _b] = ("sbuf", [128, 256], "float16")
     SCRATCH["HW%d" % _b] = ("sbuf", [128, 128], "bfloat16")
     SCRATCH["HX%d" % _b] = ("sbuf", [128, 128], "bfloat16")
     SCRATCH["BK%d" % _b] = ("psum", [128, 512], "float32")
@@ -76,7 +74,7 @@ SEMAPHORES = ["xld", "x2ld", "fill", "fz", "f2", "fp", "v", "iot", "w2ld", "own"
               "lo", "oa", "fin", "fq", "yd", "hl", "n0", "nb", "go", "kv", "rr", "rs"]
 SEMAPHORES += ["fw%d" % c for c in range(WC)] + ["wl%d" % c for c in range(WC)]
 for _b in range(NB):
-    SEMAPHORES += ["%s%d" % (n, _b) for n in ("cu", "cc", "gg", "mm", "mk", "mn", "ee", "hw", "ac")]
+    SEMAPHORES += ["%s%d" % (n, _b) for n in ("cu", "cc", "gg", "mm", "mn", "ee", "hw", "ac")]
 for _r in range(4):
     SEMAPHORES += ["pa%d" % _r, "pl%d" % _r, "ra%d" % _r]
 
@@ -127,15 +125,15 @@ def rank_program(g, core, T, topo):
 
     g.iota(T.KI[:, 0:1], [[1, 1]], 0, 1).then_inc(sem.iot, 1)
     g.iota(T.CI[:, :], [[1, 128]], 0, 0).then_inc(sem.iot, 1)
-    g.iota(T.PR[:, 0:384], [[0, 96], [1, 4]], 0, 0).then_inc(sem.fill, 1)
+    g.iota(T.PR[:, 0:384], [[0, 384]], 0, 0).then_inc(sem.fill, 1)
     g.wait_ge(sem.xld, 64)
     g.remote_dma_fused([RemoteDMATransfer(dst_ids=[d], dma_engine_mask=m, remote_sem=sem["pa%d" % rank],
                                           src=T.X[:, :], dst=T["D%d" % rank][:, :]) for s, d, m in dests],
                        local_sem=sem.psent)
     g.sem_inc(sem.go, 1)
-    g.iota(T.CM[:, :], [[0, 4], [1, 32]], -1, 0, allow_small_or_imprecise_dtypes=True).then_inc(sem.iot, 1)
+    g.iota(T.CM[:, :], [[0, 4], [1, 32]], 1, 0, allow_small_or_imprecise_dtypes=True).then_inc(sem.iot, 1)
     g.iota(T.CQ[:, :], [[1, 4], [0, 32]], 0, 0, allow_small_or_imprecise_dtypes=True).then_inc(sem.iot, 1)
-    g.iota(T.PR[:, 384:1536], [[0, 288], [1, 4]], 0, 0).then_inc(sem.fp, 1)
+    g.iota(T.PR[:, 384:1536], [[0, 1152]], 0, 0).then_inc(sem.fp, 1)
     for c in range(2, WC):
         g.iota(T.W[:, w * c:w * c + w], [[0, w]], 0, 0).then_inc(sem["fw%d" % c], 1)
 
@@ -187,8 +185,9 @@ def rank_program(g, core, T, topo):
     v(V.tensor_scalar(col(7), r_, 3.0, 2.0, OP.is_lt, OP.mult))
     v(V.tensor_scalar(col(8), r_, 6.0, None, OP.is_lt))
     v(V.tensor_scalar(col(25), r_, 12.0, 3.0, OP.is_equal, OP.mult))
+    v(V.tensor_scalar(col(55), r_, 15.0, 3.0, OP.is_equal, OP.mult))
     for at, terms in ((16, [(6, 1.0), (8, 1.0), (14, -2048.0), (12, 4096.0), (13, -2.0)]),
-                      (30, [(10, 32.0), (11, 1.0), (12, 8192.0)]),
+                      (30, [(10, -32.0), (11, -1.0)]),
                       (37, [(14, -1.0), (15, 1.0)])):
         for n, (row, c) in enumerate(terms):
             v(V.tensor_scalar(col(at + n), r_, float(row), c, OP.is_equal, OP.mult))
@@ -198,33 +197,31 @@ def rank_program(g, core, T, topo):
     v(V.tensor_scalar(col(22), r_, 7.0, None, OP.is_equal))
     v(V.tensor_scalar(col(23), r_, 9.0, None, OP.is_equal))
     v(V.tensor_scalar(col(24), r_, 12.0, None, OP.is_equal))
-    v(V.tensor_scalar(col(40), r_, 9.0, None, OP.subtract))
-    v(V.tensor_scalar(col(41), r_, 8.0, None, OP.subtract))
     vsync()
     v(V.tensor_tensor(col(36), col(34), col(35), OP.mult))
     v(V.tensor_tensor(col(9), col(7), col(8), OP.subtract))
     v(V.tensor_reduce(col(10), KF[:, 16:21], AxisListType.X, OP.add))
-    v(V.tensor_reduce(col(21), KF[:, 30:33], AxisListType.X, OP.add))
+    v(V.tensor_reduce(col(40), KF[:, 16:19], AxisListType.X, OP.add))
+    v(V.tensor_tensor(col(41), col(30), col(31), OP.add))
     v(V.tensor_tensor(col(11), col(22), col(24), OP.subtract))
     v(V.tensor_tensor(col(12), col(23), col(24), OP.subtract))
-    v(V.tensor_scalar(T.E1[:, :], T.CJ[:, 0:128:4], col(40), 2048.0, OP.is_equal, OP.mult))
-    v(V.tensor_scalar(T.E2[:, :], T.CJ[:, 0:128:4], col(41), 2048.0, OP.is_equal, OP.mult))
     v(V.tensor_scalar(T.B32[:, :], T.CG[:, :], g_, None, OP.is_equal))
     v(V.tensor_scalar(T.B8[:, :], T.CH[:, :], g_, None, OP.is_equal))
     vsync()
     v(V.tensor_tensor(col(15), col(36), col(39), OP.add))
     v(V.tensor_tensor(col(13), col(9), col(25), OP.add))
+    v(V.tensor_tensor(col(56), col(9), col(55), OP.add))
+    v(V.tensor_tensor(col(21), col(40), col(41), OP.add))
     v(V.tensor_scalar(col(26), col(11), -1.0, None, OP.mult))
     v(V.tensor_scalar(col(27), col(12), -1.0, None, OP.mult))
     v(V.tensor_scalar(col(54), col(38), -1.0, None, OP.mult))
-    v(V.tensor_tensor(T.E3[:, :], T.E2[:, :], T.E1[:, :], OP.subtract))
     vsync()
     v(V.tensor_scalar(col(28), col(13), 8192.0, None, OP.mult))
     v(V.tensor_scalar(col(29), col(13), -BIG, None, OP.mult))
-    v(V.tensor_tensor(T.E5[:, :], T.E3[:, :], T.B32[:, :], OP.mult))
+    v(V.tensor_scalar(col(57), col(56), -8192.0, None, OP.mult))
     vsync()
     half = nv[0]
-    v(V.tensor_tensor(col(53), col(28), col(20), OP.subtract))
+    v(V.tensor_tensor(col(58), col(57), col(20), OP.add))
     V.wait_ge(sem.n0, 16)
     for n in range(2):
         v(V.tensor_tensor(col(42 + n), T.N0[:, n:n + 1], col(8), OP.mult))
@@ -233,13 +230,15 @@ def rank_program(g, core, T, topo):
     for n, c in enumerate((14, 38, 37, 54)):
         v(V.tensor_scalar(KF[:, 44 + 2 * n:46 + 2 * n], T.KV[:, 2:4], col(c), col(29), OP.mult, OP.add))
     vsync()
-    v(V.tensor_scalar(T.E2[:, :], T.B32[:, :], col(53), None, OP.mult))
-    vsync()
-    v(V.tensor_tensor(T.RB[:, 32:64], T.E5[:, :], T.E2[:, :], OP.add))
+    v(V.tensor_tensor(col(53), col(52), col(58), OP.add))
     cols = nv[0]
     v(V.tensor_scalar(T.MASK[:, :], T.CJ[:, :], i_, None, OP.is_equal))
     v(V.tensor_scalar(T.IDF[:, :], T.CI[:, :], p_, None, OP.is_equal))
     v(V.tensor_scalar(T.SEL[:, :], T.CI[:, 0:32], k_, None, OP.is_equal))
+    v(V.tensor_scalar(T.NSEL[:, :], T.CI[:, 0:32], k_, -1.0, OP.is_equal, OP.mult))
+    vsync()
+    v(V.tensor_scalar(T.FIT[:, 0:128], T.MASK[:, :], -2.0 * TOP, TOP, OP.mult, OP.add))
+    v(V.tensor_scalar(T.FIT[:, 128:256], T.MASK[:, :], -TOP - 2048.0, TOP, OP.mult, OP.add))
     statics = nv[0]
 
     S.wait_ge(sem.fz, 1)
@@ -268,23 +267,24 @@ def rank_program(g, core, T, topo):
 
     S.wait_ge(sem.v, half)
     scaled("rr", T.R0[:, 0:32], T.B32[:, :], 28)
-    scaled("rr", T.R0[:, 32:64], T.B8[:, :], 29)
-    scaled("rr", T.R0[:, 64:96], T.B32[:, :], 28)
+    scaled("rr", T.R0[:, 32:64], T.B32[:, :], 57)
+    scaled("rr", T.R0[:, 64:96], T.B8[:, :], 29)
     S.wait_ge(sem.v, cols)
     for n in range(4):
         scaled("rr", T.R0[:, 96 + 8 * n:104 + 8 * n], T.B8[:, 0:8], 44 + 2 * n)
-        scaled("rr", T.R1[:, 32 + 8 * n:40 + 8 * n], T.B8[:, 0:8], 45 + 2 * n)
+        scaled("rr", T.R1[:, 64 + 8 * n:72 + 8 * n], T.B8[:, 0:8], 45 + 2 * n)
     scaled("rr", T.R1[:, 0:32], T.B32[:, :], 52)
-    scaled("rr", T.R1[:, 64:96], T.RB[:, 32:64], None)
+    scaled("rr", T.R1[:, 32:64], T.B32[:, :], 53)
     S.wait_ge(sem.v, statics)
     scaled("rs", T.ID[:, :], T.IDF[:, :], None)
     nr["rs"] += 1
     S.activation(T.NID[:, :], T.IDF[:, :], FN.Copy, scale=-1.0).then_inc(sem.rs, 1)
     scaled("rs", T.RA[:, 0:32], T.B32[:, :], 10)
-    scaled("rs", T.RA[:, 64:96], T.B32[:, :], 21)
+    scaled("rs", T.RA[:, 32:64], T.B32[:, :], 21)
     for n, c in enumerate((11, 12, 26, 27)):
-        scaled("rs", T.RA[:, 32 + 8 * n:40 + 8 * n], T.B8[:, 0:8], c)
-    scaled("rs", T.RB[:, 0:32], T.B8[:, :], 29)
+        scaled("rs", T.RA[:, 64 + 8 * n:72 + 8 * n], T.B8[:, 0:8], c)
+    scaled("rs", T.RB[:, 0:32], T.B32[:, :], 57)
+    scaled("rs", T.RB[:, 32:64], T.B8[:, :], 29)
 
     Y.wait_ge(sem.nb, 12)
     Y.wait_ge(sem.f2, 8)
@@ -329,6 +329,8 @@ def rank_program(g, core, T, topo):
         V.tensor_tensor(C[:, :], T.W[:, 0:WIN].indirect(T["CU" + B][:, :]), points, OP.is_gt).then_inc(sem["cc" + B], 1)
         S.wait_ge(sem["cu" + B], t)
         S.activation(G[:, :], T.W2[:, 0:WIN2].indirect(T["CU" + B][:, :]), FN.Copy).then_inc(sem["gg" + B], 1)
+        if x == NB:
+            PE.wait_ge(sem.rs, nr["rs"])
         PE.wait_ge(sem["gg" + B], t)
         for i in range(4):
             PE.matmul(bank[:, i:384:4], G[:, i::4], T.RA[:, :], i == 0, False).then_inc(sem["mm" + B], 1)
@@ -339,24 +341,21 @@ def rank_program(g, core, T, topo):
     def move(x):
         t, b = divmod(x, NB)
         B = str(b)
-        bank = T["BK" + B]
         if t == STEPS - 1:
             return
         V.wait_ge(sem["mm" + B], 8 * (t + 1))
-        V.tensor_tensor(T["AM" + B][:, :], bank[:, 0:128], T.MASK[:, :], OP.mult).then_inc(sem["mk" + B], 1)
-        V.wait_ge(sem["mk" + B], t + 1)
-        V.tensor_tensor(T["IN" + B][:, :], bank[:, 256:384], T["AM" + B][:, :], OP.min).then_inc(sem["mn" + B], 1)
+        V.tensor_tensor(T["IN" + B][:, :], T["BK" + B][:, 0:256], T.FIT[:, :], OP.max).then_inc(sem["mn" + B], 1)
         PE.wait_ge(sem["mn" + B], t + 1)
-        PE.matmul(T["CP" + B][:, 0:32], T["IN" + B][:, :], T.SEL[:, :], True, True).then_inc(sem["ee" + B], 1)
+        PE.matmul(T["CP" + B][:, 0:32], T["IN" + B][:, 0:128], T.SEL[:, :], True, False).then_inc(sem["ee" + B], 1)
+        PE.matmul(T["CP" + B][:, 0:32], T["IN" + B][:, 128:256], T.NSEL[:, :], False, True).then_inc(sem["ee" + B], 1)
 
     def cast(x):
         t, b = divmod(x, NB)
         B = str(b)
         if t == STEPS - 1:
             return
-        V.wait_ge(sem["ee" + B], t + 1)
-        V.tensor_scalar(T["CU" + B][:, :], T["CP" + B][:, 0:32], 2048.0, float(M), OP.add, OP.min
-                        ).then_inc(sem["cu" + B], 1)
+        V.wait_ge(sem["ee" + B], 2 * t + 2)
+        V.tensor_scalar(T["CU" + B][:, :], T["CP" + B][:, 0:32], float(M), None, OP.min).then_inc(sem["cu" + B], 1)
 
     def acc(b):
         return T.AC1[:, 0:64] if b == NB - 1 else T.AC0[:, 64 * b:64 * b + 64]
@@ -371,7 +370,7 @@ def rank_program(g, core, T, topo):
         if t:
             S.wait_ge(sem["ac" + B], 2 + 2 * t)
         todo = [T["HW" + B]]
-        S.activation(T["HW" + B][:, :], T["BK" + B][:, 128:256], FN.Relu).then_inc(sem["hw" + B], 1)
+        S.activation(T["HW" + B][:, :], T["BK" + B][:, 256:384], FN.Relu).then_inc(sem["hw" + B], 1)
         if t == 0:
             todo.append(T["HX" + B])
             S.activation(T["HX" + B][:, :], T["BK" + B][:, 384:512], FN.Relu).then_inc(sem["hw" + B], 1)
@@ -384,10 +383,12 @@ def rank_program(g, core, T, topo):
 
     total = NB * STEPS
     for x in range(total + 2):
+        if 0 <= x - 2 < total and x >= total:
+            cast(x - 2)
         if x < total:
             gather(x)
-        if 0 <= x - 2 < total:
-            cast(x - 2)
+            if 0 <= x - 2:
+                cast(x - 2)
         if 0 <= x - 1 < total:
             move(x - 1)
         if 0 <= x - 2 < total:

from concourse.bass import DstId, RemoteDMATransfer
from concourse.mybir import dt, AluOpType, AxisListType, ActivationFunctionType

OP = AluOpType
FN = ActivationFunctionType
NB = 3
NL = 512
STEPS = 15
M = 4096
WIN = 4104
WIN2 = 4112
WC = 4
EPD = 4
BIG = 262144.0
TOP = 57344.0

SCRATCH = {
    "W": ("sbuf", [128, WIN], "int32"),
    "W2": ("sbuf", [128, WIN2], "bfloat16"),
    "Z": ("sbuf", [128, 512], "bfloat16"),
    "X": ("dram", [128, 96], "int32"),
    "N0": ("sbuf", [128, 2], "int32"),
    "KV": ("sbuf", [128, 4], "bfloat16"),
    "P": ("sbuf", [128, NB * NL], "int32"),
    "CM": ("sbuf", [128, 128], "float32"),
    "CQ": ("sbuf", [128, 128], "float32"),
    "X2": ("sbuf", [128, 512], "int32"),
    "HI": ("sbuf", [128, 512], "bfloat16"),
    "LO": ("sbuf", [128, 512], "bfloat16"),
    "NHB": ("sbuf", [128, 512], "bfloat16"),
    "NLB": ("sbuf", [128, 512], "bfloat16"),
    "PR": ("sbuf", [128, 4 * 384], "int32"),
    "CI": ("sbuf", [128, 128], "int32"),
    "CJ": ("sbuf", [128, 128], "int32"),
    "CG": ("sbuf", [128, 32], "int32"),
    "CH": ("sbuf", [128, 32], "int32"),
    "KI": ("sbuf", [128, 16], "int32"),
    "KB": ("sbuf", [128, 8], "float32"),
    "KF": ("sbuf", [128, 64], "float32"),
    "ID": ("sbuf", [128, 128], "bfloat16"),
    "NID": ("sbuf", [128, 128], "bfloat16"),
    "IDF": ("sbuf", [128, 128], "float32"),
    "MASK": ("sbuf", [128, 128], "float32"),
    "FIT": ("sbuf", [128, 256], "float32"),
    "B32": ("sbuf", [128, 32], "float32"),
    "B8": ("sbuf", [128, 32], "float32"),
    "SEL": ("sbuf", [128, 32], "float16"),
    "NSEL": ("sbuf", [128, 32], "float16"),
    "RA": ("sbuf", [128, 96], "bfloat16"),
    "RB": ("sbuf", [128, 64], "bfloat16"),
    "R0": ("sbuf", [128, 128], "bfloat16"),
    "R1": ("sbuf", [128, 96], "bfloat16"),
    "OUT": ("sbuf", [128, 96], "float32"),
    "TMP": ("sbuf", [128, 96], "float32"),
    "SUM": ("sbuf", [128, 24], "float32"),
    "YS": ("sbuf", [128, 128], "float32"),
    "AC0": ("psum", [128, 512], "float32"),
    "AC1": ("psum", [128, 512], "float32"),
}
for _b in range(NB):
    SCRATCH["C%d" % _b] = ("sbuf", [128, NL], "bfloat16")
    SCRATCH["G%d" % _b] = ("sbuf", [128, NL], "bfloat16")
    SCRATCH["CU%d" % _b] = ("sbuf", [128, 32], "uint16")
    SCRATCH["IN%d" % _b] = ("sbuf", [128, 256], "float16")
    SCRATCH["HW%d" % _b] = ("sbuf", [128, 128], "bfloat16")
    SCRATCH["HX%d" % _b] = ("sbuf", [128, 128], "bfloat16")
    SCRATCH["BK%d" % _b] = ("psum", [128, 512], "float32")
    SCRATCH["CP%d" % _b] = ("psum", [128, 512], "float32")
for _r in range(4):
    SCRATCH["D%d" % _r] = ("dram", [128, 96], "int32")
    SCRATCH["L%d" % _r] = ("sbuf", [128, 24], "float32")

SEMAPHORES = ["xld", "x2ld", "fill", "fz", "f2", "fp", "v", "iot", "w2ld", "own", "psent", "rsent",
              "lo", "oa", "fin", "fq", "yd", "hl", "n0", "nb", "go", "kv", "rr", "rs"]
SEMAPHORES += ["fw%d" % c for c in range(WC)] + ["wl%d" % c for c in range(WC)]
for _b in range(NB):
    SEMAPHORES += ["%s%d" % (n, _b) for n in ("cu", "cc", "gg", "mm", "mn", "ee", "hw", "ac")]
for _r in range(4):
    SEMAPHORES += ["pa%d" % _r, "pl%d" % _r, "ra%d" % _r]


def rank_program(g, core, T, topo):
    rank = T.rank_of(core)
    if rank is None:
        return
    sem = T.sem
    V, S, PE, Y = g.vector, g.scalar, g.tensor, g.sync
    n_ranks = len(T.cores)
    peers = [(rank + s) % n_ranks for s in range(1, n_ranks)]

    order = sorted(range(1, n_ranks), key=lambda s: topo.die(T.cores[(rank + s) % n_ranks]) == topo.die(core))
    dests = []
    for n, s in enumerate(order):
        c = T.cores[(rank + s) % n_ranks]
        e = topo.engines(core, c)
        e = (e[0::2] + e[1::2])[EPD * n:EPD * n + EPD]
        rid, pid, _se = topo.addr(c)
        dests.append((s, DstId(rid=rid, pnc=pid), sum(1 << x for x in e)))

    for a in range(4):
        Y.dma_start(T.X[32 * a:32 * a + 32, :], T.pts[a % 3::3, :]).then_inc(sem.xld, 16)
    Y.dma_start(T.X2[0:64, :], T.nodes[6::16, :]).then_inc(sem.x2ld, 16)
    Y.dma_start(T.X2[64:128, :], T.nodes[7::16, :]).then_inc(sem.x2ld, 16)
    Y.dma_start(T.N0[:, :], T.nodes[:, 0:2]).then_inc(sem.n0, 16)
    Y.wait_ge(sem.fill, 1)
    for a in range(6):
        Y.dma_start(T.PR[a::16, 0:384], T.pts[a % 3::3, :]).then_inc(sem.own, 16)
    w = M // WC

    def load(c):
        Y.wait_ge(sem["fw%d" % c], 1)
        for a in range(6):
            Y.dma_start(T.W[a::16, w * c:w * c + w], T.nodes[a::16, w * c:w * c + w]).then_inc(sem["wl%d" % c], 16)

    Y.wait_ge(sem.go, 1)
    load(0)
    Y.wait_ge(sem.fp, 1)
    for s, r in enumerate(peers):
        Y.wait_ge(sem["pa%d" % r], EPD)
        for a in range(6):
            Y.dma_start(T.PR[a::16, 384 * (s + 1):384 * (s + 2)],
                        T["D%d" % r][32 * (a % 3):32 * (a % 3) + 32, :]).then_inc(sem["pl%d" % r], 16)
    load(1)
    load(2)

    g.iota(T.KI[:, 0:1], [[1, 1]], 0, 1).then_inc(sem.iot, 1)
    g.iota(T.CI[:, :], [[1, 128]], 0, 0).then_inc(sem.iot, 1)
    g.iota(T.PR[:, 0:384], [[0, 384]], 0, 0).then_inc(sem.fill, 1)
    g.wait_ge(sem.xld, 64)
    g.remote_dma_fused([RemoteDMATransfer(dst_ids=[d], dma_engine_mask=m, remote_sem=sem["pa%d" % rank],
                                          src=T.X[:, :], dst=T["D%d" % rank][:, :]) for s, d, m in dests],
                       local_sem=sem.psent)
    g.sem_inc(sem.go, 1)
    g.iota(T.CM[:, :], [[0, 4], [1, 32]], 1, 0, allow_small_or_imprecise_dtypes=True).then_inc(sem.iot, 1)
    g.iota(T.CQ[:, :], [[1, 4], [0, 32]], 0, 0, allow_small_or_imprecise_dtypes=True).then_inc(sem.iot, 1)
    g.iota(T.PR[:, 384:1536], [[0, 1152]], 0, 0).then_inc(sem.fp, 1)
    for c in range(2, WC):
        g.iota(T.W[:, w * c:w * c + w], [[0, w]], 0, 0).then_inc(sem["fw%d" % c], 1)

    nv = [0]

    def v(ins):
        nv[0] += 1
        ins.then_inc(sem.v, 1)

    def vsync():
        V.wait_ge(sem.v, nv[0])

    KF = T.KF

    def col(j):
        return KF[:, j:j + 1]

    v(V.memset(T.Z[:, :], 0.0))
    v(V.memset(KF[:, :], 0.0))
    v(V.memset(T.KV[:, :], 0.0))
    V.wait_ge(sem.iot, 2)
    v(V.tensor_scalar(T.KI[:, 1:2], T.KI[:, 0:1], 15, None, OP.bitwise_and))
    v(V.tensor_scalar(T.KI[:, 2:3], T.KI[:, 0:1], 4, None, OP.arith_shift_right))
    v(V.tensor_scalar(T.KI[:, 3:4], T.KI[:, 0:1], 3, None, OP.bitwise_and))
    v(V.tensor_scalar(T.KI[:, 4:5], T.KI[:, 0:1], 2, None, OP.arith_shift_right))
    v(V.tensor_scalar(T.KI[:, 5:6], T.KI[:, 0:1], 7, None, OP.bitwise_and))
    vsync()
    v(V.tensor_copy(KF[:, 0:6], T.KI[:, 0:6]))
    vsync()
    base = nv[0]
    p_, r_, g_, i_, k_ = [col(j) for j in range(5)]
    v(V.tensor_scalar(col(14), r_, 14.0, None, OP.is_equal))
    vsync()
    V.tensor_scalar(T.Z[:, :], T.Z[:, :], col(14), None, OP.add).then_inc(sem.fz, 1)
    V.memset(T.W[:, 0:w], 0).then_inc(sem.fw0, 1)

    V.wait_ge(sem.x2ld, 32)
    v(V.tensor_copy(T.HI[:, :], T.X2[:, :]))
    vsync()
    v(V.tensor_tensor(T.LO[:, :], T.X2[:, :], T.HI[:, :], OP.subtract))
    hilo = nv[0]
    V.memset(T.W[:, w:2 * w], 0).then_inc(sem.fw1, 1)
    v(V.memset(T.W2[:, M:WIN2], 1.0))
    v(V.memset(T.W[:, M:WIN], 0))

    v(V.tensor_scalar(T.CJ[:, :], T.CI[:, :], 2, 3, OP.arith_shift_right, OP.bitwise_and))
    v(V.tensor_scalar(T.CG[:, :], T.CI[:, 0:32], 2, None, OP.arith_shift_right))
    v(V.tensor_scalar(T.CH[:, :], T.CI[:, 0:32], 7, None, OP.bitwise_and))
    v(V.tensor_scalar(col(7), r_, 3.0, 2.0, OP.is_lt, OP.mult))
    v(V.tensor_scalar(col(8), r_, 6.0, None, OP.is_lt))
    v(V.tensor_scalar(col(25), r_, 12.0, 3.0, OP.is_equal, OP.mult))
    v(V.tensor_scalar(col(55), r_, 15.0, 3.0, OP.is_equal, OP.mult))
    for at, terms in ((16, [(6, 1.0), (8, 1.0), (14, -2048.0), (12, 4096.0), (13, -2.0)]),
                      (30, [(10, -32.0), (11, -1.0)]),
                      (37, [(14, -1.0), (15, 1.0)])):
        for n, (row, c) in enumerate(terms):
            v(V.tensor_scalar(col(at + n), r_, float(row), c, OP.is_equal, OP.mult))
    v(V.tensor_scalar(col(34), r_, -1.0, 9.0, OP.mult, OP.add))
    v(V.tensor_scalar(col(35), r_, 6.0, None, OP.is_ge))
    v(V.tensor_scalar(col(39), r_, 3.0, -1.0, OP.is_ge, OP.mult))
    v(V.tensor_scalar(col(22), r_, 7.0, None, OP.is_equal))
    v(V.tensor_scalar(col(23), r_, 9.0, None, OP.is_equal))
    v(V.tensor_scalar(col(24), r_, 12.0, None, OP.is_equal))
    vsync()
    v(V.tensor_tensor(col(36), col(34), col(35), OP.mult))
    v(V.tensor_tensor(col(9), col(7), col(8), OP.subtract))
    v(V.tensor_reduce(col(10), KF[:, 16:21], AxisListType.X, OP.add))
    v(V.tensor_reduce(col(40), KF[:, 16:19], AxisListType.X, OP.add))
    v(V.tensor_tensor(col(41), col(30), col(31), OP.add))
    v(V.tensor_tensor(col(11), col(22), col(24), OP.subtract))
    v(V.tensor_tensor(col(12), col(23), col(24), OP.subtract))
    v(V.tensor_scalar(T.B32[:, :], T.CG[:, :], g_, None, OP.is_equal))
    v(V.tensor_scalar(T.B8[:, :], T.CH[:, :], g_, None, OP.is_equal))
    vsync()
    v(V.tensor_tensor(col(15), col(36), col(39), OP.add))
    v(V.tensor_tensor(col(13), col(9), col(25), OP.add))
    v(V.tensor_tensor(col(56), col(9), col(55), OP.add))
    v(V.tensor_tensor(col(21), col(40), col(41), OP.add))
    v(V.tensor_scalar(col(26), col(11), -1.0, None, OP.mult))
    v(V.tensor_scalar(col(27), col(12), -1.0, None, OP.mult))
    v(V.tensor_scalar(col(54), col(38), -1.0, None, OP.mult))
    vsync()
    v(V.tensor_scalar(col(28), col(13), 8192.0, None, OP.mult))
    v(V.tensor_scalar(col(29), col(13), -BIG, None, OP.mult))
    v(V.tensor_scalar(col(57), col(56), -8192.0, None, OP.mult))
    vsync()
    half = nv[0]
    v(V.tensor_tensor(col(58), col(57), col(20), OP.add))
    V.wait_ge(sem.n0, 16)
    for n in range(2):
        v(V.tensor_tensor(col(42 + n), T.N0[:, n:n + 1], col(8), OP.mult))
    V.wait_ge(sem.kv, 64)
    v(V.tensor_tensor(col(52), T.KV[:, 1:2], col(18), OP.add))
    for n, c in enumerate((14, 38, 37, 54)):
        v(V.tensor_scalar(KF[:, 44 + 2 * n:46 + 2 * n], T.KV[:, 2:4], col(c), col(29), OP.mult, OP.add))
    vsync()
    v(V.tensor_tensor(col(53), col(52), col(58), OP.add))
    cols = nv[0]
    v(V.tensor_scalar(T.MASK[:, :], T.CJ[:, :], i_, None, OP.is_equal))
    v(V.tensor_scalar(T.IDF[:, :], T.CI[:, :], p_, None, OP.is_equal))
    v(V.tensor_scalar(T.SEL[:, :], T.CI[:, 0:32], k_, None, OP.is_equal))
    v(V.tensor_scalar(T.NSEL[:, :], T.CI[:, 0:32], k_, -1.0, OP.is_equal, OP.mult))
    vsync()
    v(V.tensor_scalar(T.FIT[:, 0:128], T.MASK[:, :], -2.0 * TOP, TOP, OP.mult, OP.add))
    v(V.tensor_scalar(T.FIT[:, 128:256], T.MASK[:, :], -TOP - 2048.0, TOP, OP.mult, OP.add))
    statics = nv[0]

    S.wait_ge(sem.fz, 1)
    for c in range(3):
        S.activation(T.W2[:, c * 512:c * 512 + 512], T.Z[:, :], FN.Copy).then_inc(sem.f2, 1)
    S.wait_ge(sem.v, hilo)
    for row, c, src in ((12, 0, T.HI[0:64:8, 0:2]), (13, 0, T.LO[0:64:8, 0:2]),
                        (14, 2, T.HI[64:128:8, 0:2]), (15, 2, T.LO[64:128:8, 0:2])):
        S.dma_start(T.KV[row::16, c:c + 2], src).then_inc(sem.kv, 16)
    S.wait_ge(sem.v, base)
    S.wait_ge(sem.iot, 4)
    for u in range(4):
        S.activation(T.KB[0:64, u:u + 1], KF[0:64, 5:6], FN.Copy, bias=4.0 * u, scale=16.0).then_inc(sem.nb, 1)
        S.activation(T.NLB[0:64, 128 * u:128 * u + 128], T.CM[0:64, :], FN.Copy).then_inc(sem.nb, 1)
    S.wait_ge(sem.nb, 8)
    for u in range(4):
        S.activation(T.NHB[0:64, 128 * u:128 * u + 128], T.CQ[0:64, :], FN.Identity, bias=T.KB[0:64, u:u + 1]
                     ).then_inc(sem.nb, 1)
    for c in range(3, 8):
        S.activation(T.W2[:, c * 512:c * 512 + 512], T.Z[:, :], FN.Copy).then_inc(sem.f2, 1)
    nr = {"rr": 0, "rs": 0}

    def scaled(name, out, mask, c):
        nr[name] += 1
        S.activation(out, mask, FN.Copy, scale=1.0 if c is None else col(c)).then_inc(sem[name], 1)

    S.wait_ge(sem.v, half)
    scaled("rr", T.R0[:, 0:32], T.B32[:, :], 28)
    scaled("rr", T.R0[:, 32:64], T.B32[:, :], 57)
    scaled("rr", T.R0[:, 64:96], T.B8[:, :], 29)
    S.wait_ge(sem.v, cols)
    for n in range(4):
        scaled("rr", T.R0[:, 96 + 8 * n:104 + 8 * n], T.B8[:, 0:8], 44 + 2 * n)
        scaled("rr", T.R1[:, 64 + 8 * n:72 + 8 * n], T.B8[:, 0:8], 45 + 2 * n)
    scaled("rr", T.R1[:, 0:32], T.B32[:, :], 52)
    scaled("rr", T.R1[:, 32:64], T.B32[:, :], 53)
    S.wait_ge(sem.v, statics)
    scaled("rs", T.ID[:, :], T.IDF[:, :], None)
    nr["rs"] += 1
    S.activation(T.NID[:, :], T.IDF[:, :], FN.Copy, scale=-1.0).then_inc(sem.rs, 1)
    scaled("rs", T.RA[:, 0:32], T.B32[:, :], 10)
    scaled("rs", T.RA[:, 32:64], T.B32[:, :], 21)
    for n, c in enumerate((11, 12, 26, 27)):
        scaled("rs", T.RA[:, 64 + 8 * n:72 + 8 * n], T.B8[:, 0:8], c)
    scaled("rs", T.RB[:, 0:32], T.B32[:, :], 57)
    scaled("rs", T.RB[:, 32:64], T.B8[:, :], 29)

    Y.wait_ge(sem.nb, 12)
    Y.wait_ge(sem.f2, 8)
    Y.wait_ge(sem.v, hilo)
    for row, src in ((6, T.HI[0:64, :]), (7, T.HI[64:128, :]), (8, T.LO[0:64, :]), (9, T.LO[64:128, :]),
                     (11, T.NLB[0:64, :]), (10, T.NHB[0:64, :])):
        Y.dma_start(T.W2[row::16, 0:M], src).then_inc(sem.w2ld, 16)
    load(3)

    for s in range(n_ranks):
        if s == 0:
            V.wait_ge(sem.own, 96)
        else:
            V.wait_ge(sem["pl%d" % peers[s - 1]], 96)
        v(V.tensor_scalar(T.P[:, s::4], T.PR[:, 384 * s:384 * s + 384], col(15), None, OP.add))
    vsync()

    PE.wait_ge(sem.v, statics)
    PE.wait_ge(sem.rr, nr["rr"])

    def gather(x):
        t, b = divmod(x, NB)
        B = str(b)
        points = T.P[:, NL * b:NL * b + NL]
        bank = T["BK" + B]
        C, G = T["C" + B], T["G" + B]
        if t == 0:
            V.tensor_scalar(G[:, :], points, col(42), None, OP.is_lt).then_inc(sem["cc" + B], 1)
            V.tensor_scalar(C[:, :], points, col(43), None, OP.is_lt).then_inc(sem["cc" + B], 1)
            PE.wait_ge(sem["cc" + B], 1)
            for i in range(4):
                PE.matmul(bank[:, i:512:4], G[:, i::4], T.R0[:, :], i == 0, False).then_inc(sem["mm" + B], 1)
            PE.wait_ge(sem["cc" + B], 2)
            for i in range(4):
                PE.matmul(bank[:, i:384:4], C[:, i::4], T.R1[:, :], False, i == 3).then_inc(sem["mm" + B], 1)
            return
        if x == NB:
            for c in range(WC):
                V.wait_ge(sem["wl%d" % c], 96)
            S.wait_ge(sem.w2ld, 96)
        V.wait_ge(sem["cu" + B], t)
        V.tensor_tensor(C[:, :], T.W[:, 0:WIN].indirect(T["CU" + B][:, :]), points, OP.is_gt).then_inc(sem["cc" + B], 1)
        S.wait_ge(sem["cu" + B], t)
        S.activation(G[:, :], T.W2[:, 0:WIN2].indirect(T["CU" + B][:, :]), FN.Copy).then_inc(sem["gg" + B], 1)
        if x == NB:
            PE.wait_ge(sem.rs, nr["rs"])
        PE.wait_ge(sem["gg" + B], t)
        for i in range(4):
            PE.matmul(bank[:, i:384:4], G[:, i::4], T.RA[:, :], i == 0, False).then_inc(sem["mm" + B], 1)
        PE.wait_ge(sem["cc" + B], t + 2)
        for i in range(4):
            PE.matmul(bank[:, 128 + i:384:4], C[:, i::4], T.RB[:, :], False, i == 3).then_inc(sem["mm" + B], 1)

    def move(x):
        t, b = divmod(x, NB)
        B = str(b)
        if t == STEPS - 1:
            return
        V.wait_ge(sem["mm" + B], 8 * (t + 1))
        V.tensor_tensor(T["IN" + B][:, :], T["BK" + B][:, 0:256], T.FIT[:, :], OP.max).then_inc(sem["mn" + B], 1)
        PE.wait_ge(sem["mn" + B], t + 1)
        PE.matmul(T["CP" + B][:, 0:32], T["IN" + B][:, 0:128], T.SEL[:, :], True, False).then_inc(sem["ee" + B], 1)
        PE.matmul(T["CP" + B][:, 0:32], T["IN" + B][:, 128:256], T.NSEL[:, :], False, True).then_inc(sem["ee" + B], 1)

    def cast(x):
        t, b = divmod(x, NB)
        B = str(b)
        if t == STEPS - 1:
            return
        V.wait_ge(sem["ee" + B], 2 * t + 2)
        V.tensor_scalar(T["CU" + B][:, :], T["CP" + B][:, 0:32], float(M), None, OP.min).then_inc(sem["cu" + B], 1)

    def acc(b):
        return T.AC1[:, 0:64] if b == NB - 1 else T.AC0[:, 64 * b:64 * b + 64]

    def weigh(x):
        t, b = divmod(x, NB)
        B = str(b)
        if t == STEPS - 1:
            S.wait_ge(sem["mm" + B], 8 * (t + 1))
        else:
            S.wait_ge(sem["mn" + B], t + 1)
        if t:
            S.wait_ge(sem["ac" + B], 2 + 2 * t)
        todo = [T["HW" + B]]
        S.activation(T["HW" + B][:, :], T["BK" + B][:, 256:384], FN.Relu).then_inc(sem["hw" + B], 1)
        if t == 0:
            todo.append(T["HX" + B])
            S.activation(T["HX" + B][:, :], T["BK" + B][:, 384:512], FN.Relu).then_inc(sem["hw" + B], 1)
        if x == 0:
            PE.wait_ge(sem.rs, nr["rs"])
        PE.wait_ge(sem["hw" + B], t + 2)
        for n, h in enumerate(todo):
            PE.matmul(acc(b), T.ID[:, :], h[:, 0:64], t == 0 and n == 0 and b != 1, False).then_inc(sem["ac" + B], 1)
            PE.matmul(acc(b), T.NID[:, :], h[:, 64:128], False, t == STEPS - 1 and b != 0).then_inc(sem["ac" + B], 1)

    total = NB * STEPS
    for x in range(total + 2):
        if 0 <= x - 2 < total and x >= total:
            cast(x - 2)
        if x < total:
            gather(x)
            if 0 <= x - 2:
                cast(x - 2)
        if 0 <= x - 1 < total:
            move(x - 1)
        if 0 <= x - 2 < total:
            weigh(x - 2)

    for b in range(NB):
        for bb in ([0, 1] if b < NB - 1 else [2]):
            S.wait_ge(sem["ac%d" % bb], 2 + 2 * STEPS)
            V.wait_ge(sem["ac%d" % bb], 2 + 2 * STEPS)
        S.activation(T.TMP[:, 32 * b:32 * b + 32], acc(b)[:, 32:64], FN.Copy).then_inc(sem.lo, 1)
        V.wait_ge(sem.lo, max(b + 1, 2))
        for s in range(n_ranks):
            V.tensor_tensor(T.OUT[:, 24 * s + 8 * b:24 * s + 8 * b + 8], acc(b)[:, s:32:4],
                            T.TMP[:, 32 * b + s:32 * b + 32:4], OP.add).then_inc(sem.oa, 1)
    g.wait_ge(sem.oa, NB * n_ranks)
    g.remote_dma_fused([RemoteDMATransfer(dst_ids=[d], dma_engine_mask=m, remote_sem=sem["ra%d" % rank],
                                          src=T.OUT[:, 24 * s:24 * s + 24], dst=T["L%d" % rank][:, :])
                        for s, d, m in dests], local_sem=sem.rsent)
    V.wait_ge(sem.oa, NB * n_ranks)
    prev = T.OUT[:, 0:24]
    for n, r in enumerate(peers):
        V.wait_ge(sem["ra%d" % r], EPD)
        if n:
            V.wait_ge(sem.fin, n)
        V.tensor_tensor(T.SUM[:, :], prev, T["L%d" % r][:, :], OP.add).then_inc(sem.fin, 1)
        prev = T.SUM[:, :]
    PE.wait_ge(sem.fin, 3)
    PE.matmul(T.BK0[0:24, 0:128], T.SUM[:, :], T.IDF[:, :], True, True).then_inc(sem.fq, 1)
    V.wait_ge(sem.fq, 1)
    V.tensor_copy(T.YS[0:24, :], T.BK0[0:24, 0:128]).then_inc(sem.hl, 1)
    for b, q in enumerate((Y, S, Y)):
        q.wait_ge(sem.hl, 1)
        q.dma_start(T.y[:, 128 * b:128 * b + 128], T.YS[8 * b:8 * b + 8, :]).then_inc(sem.yd, 16)
    Y.wait_ge(sem.yd, 48)
    g.wait_ge(sem.psent, 3 * EPD)
    g.wait_ge(sem.rsent, 3 * EPD)
